import numpy as np
import ml_dtypes


def mxq(x, axis, fmt="e4m3"):
    dtype, down = {"e4m3": (ml_dtypes.float8_e4m3fn, 7), "e5m2": (ml_dtypes.float8_e5m2, 14)}[fmt]
    v = np.moveaxis(np.asarray(x, np.float32).astype(ml_dtypes.bfloat16).astype(np.float64), axis, -1)
    blocks = v.reshape(v.shape[:-1] + (-1, 32))
    amax = np.abs(blocks).max(-1, keepdims=True)
    byte = np.maximum(np.where(amax > 0, np.frexp(amax)[1] - 1 + 127, 0) - down, 1)
    scale = np.exp2(byte - 127.0)
    codes = (blocks / scale).astype(np.float32).astype(dtype).astype(np.float64)
    return np.moveaxis((codes * scale).reshape(v.shape), -1, axis)


WIDE = False


def mx_kscale(k):
    if not WIDE:
        return np.ones(k)
    levels = np.array([10, -10, 5, -5, 0])
    if k % 512:
        return np.exp2(np.random.permutation(np.resize(levels, k // 32))).repeat(32)
    a = np.empty((k // 512, 16))
    for p in range(k // 512):
        a[p, :8] = np.random.permutation(np.resize(levels, 8))
        for g in range(8):
            far = levels[np.abs(levels - a[p, g]) >= 10]
            a[p, g + 8] = far[np.random.randint(len(far))]
    return np.exp2(a.ravel()).repeat(32)


def f64(x):
    return np.asarray(x).astype(np.float64)


def striped(idx):
    return np.tile(idx.reshape(-1, 16).T, (8, 1)).astype(np.uint16)


def unstriped(offs):
    return offs[:16].T.reshape(-1).astype(np.int64)


E2M1 = np.array([0.0, 0.5, 1.0, 1.5, 2.0, 3.0, 4.0, 6.0, -0.0, -0.5, -1.0, -1.5, -2.0, -3.0, -4.0, -6.0])


def pack_fp4(w):
    k, n = w.shape
    w = f64(np.asarray(w, np.float32).astype(ml_dtypes.bfloat16)).reshape(k // 32, 32, n)
    amax = np.abs(w).max(1)
    mant, ex = np.frexp(amax / 6.0)
    byte = np.clip(np.where(amax > 0, np.where(mant > 0.5, ex, ex - 1) + 127, 1), 1, 254)
    scaled = (w * np.exp2(127.0 - byte)[:, None, :]).reshape(k, n).astype(np.float32)
    c = np.ascontiguousarray(scaled.reshape(k // 512, 128, 4, n).transpose(0, 1, 3, 2)).astype(ml_dtypes.float4_e2m1fn).view(np.uint8) & 0xF
    words = (c[..., 0::2] | (c[..., 1::2] << 4)).reshape(k // 512, 128, 2 * n)
    return np.ascontiguousarray(words), np.ascontiguousarray(byte.astype(np.uint8).reshape(k // 512, 16, n))


def unpack_fp4(words, scales):
    g, _, n = scales.shape
    words = np.ascontiguousarray(words).reshape(g, 128, n, 2)
    nib = np.empty((g, 128, n, 4), np.uint8)
    nib[..., 0::2] = words & 0xF
    nib[..., 1::2] = words >> 4
    vals = E2M1[nib] * np.repeat(np.exp2(scales.astype(np.float64) - 127.0), 8, axis=1)[..., None]
    return vals.transpose(0, 1, 3, 2).reshape(g * 512, n)


def relu(v):
    return np.maximum(v, 0.0)

def planes(y):
    n, m = y.shape
    v = y.astype(np.float32).astype(ml_dtypes.bfloat16).astype(np.float64).reshape(n // 32, 32, m)
    top = np.abs(v).max(1)
    byte = np.clip(np.where(top > 0, np.frexp(top)[1] - 1 + 127 - 7, 1), 1, 254)
    codes = (v * np.exp2(127.0 - byte)[:, None, :]).reshape(n, m).astype(np.float32).astype(ml_dtypes.float8_e4m3fn).view(np.uint8)
    words = codes.reshape(n // 512, 128, 4, m).transpose(0, 1, 3, 2)
    return np.ascontiguousarray(words), np.ascontiguousarray(byte.astype(np.uint8).reshape(n // 512, 16, m))


K, T, N = 1024, 512, 512


def setup_inputs():
    n = np.random.standard_normal
    s = mx_kscale(K)[:, None]
    packed_xT = pack_fp4(n((K, T)) * s)
    return {
        "x_words": packed_xT[0],
        "x_scales": packed_xT[1],
        "w1": (n((K, N)) / np.sqrt(K) / s).astype(np.float32),
        "w2": (n((K, N)) / np.sqrt(K) / s).astype(np.float32),
        "w3": (n((K, N)) / np.sqrt(K) / s).astype(np.float32),
        "pos1": striped(np.random.permutation(T)),
        "pos2": striped(np.random.permutation(T)),
        "pos3": striped(np.random.permutation(T)),
    }


def reference(x_words, x_scales, w1, w2, w3, pos1, pos2, pos3):
    xq = unpack_fp4(x_words, x_scales)
    h = mxq(f64(w3), 0, "e4m3").T @ xq
    g = mxq(f64(w1), 0, "e4m3").T @ xq
    s = mxq(f64(w2), 0, "e4m3").T @ xq
    out_0 = relu(h[:, unstriped(pos1)] * g + s) + relu(h[:, unstriped(pos2)] * g + s) + relu(h[:, unstriped(pos3)] * g + s)
    return (out_0,) + planes(out_0)

@@ -1,0 +1,236 @@
+from contextlib import ExitStack
+
+import concourse.mybir as mybir
+from concourse.masks import make_identity
+
+K, T, N = 1024, 512, 512
+FLOPS = 3 * 2 * K * T * N
+
+F32 = mybir.dt.float32
+BF16 = mybir.dt.bfloat16
+I32 = mybir.dt.int32
+U32 = mybir.dt.uint32
+U16 = mybir.dt.uint16
+U8 = mybir.dt.uint8
+FP8X4 = mybir.dt.float8_e4m3fn_x4
+FP4X4 = mybir.dt.float4_e2m1fn_x4
+ALU = mybir.AluOpType
+RELU = mybir.ActivationFunctionType.Relu
+
+P = 128
+PACK = 4
+PASSES = K // (P * PACK)
+BLOCKS = N // P
+VB = T // P
+SPARE = 16
+Q = P // PACK
+
+
+def tile_picked_wfilmg_relu_lo_kernel(
+    tc, x_words, x_scales, w1, w2, w3, pos1, pos2, pos3, out_0, out_1, out_2
+):
+    nc = tc.nc
+    with ExitStack() as ctx:
+        keep = ctx.enter_context(tc.tile_pool(name="keep", bufs=1))
+        ring = ctx.enter_context(tc.tile_pool(name="ring", bufs=3))
+        ps_mm = ctx.enter_context(tc.psum_pool(name="ps_mm", bufs=1))
+        ps_t = ctx.enter_context(tc.psum_pool(name="ps_t", bufs=3))
+        ps_y = ctx.enter_context(tc.psum_pool(name="ps_y", bufs=2))
+
+        lists = [keep.tile([P, T // 16], U16, name=f"list{d}") for d in range(3)]
+        xw = keep.tile([P, PASSES, 2 * T], U8, name="xw", align_bytes=64)
+        xs = keep.tile([P, PASSES, T], U8, name="xs", align_bytes=64)
+        ident = keep.tile([P, P], F32, name="ident")
+        warm = keep.tile([P, 8], F32, name="warm")
+        warm2 = keep.tile([P, 8], F32, name="warm2")
+
+        nc.vector.memset(xs[:].rearrange("p z c -> p (z c)").bitcast(I32), 0)
+        nc.vector.memset(warm[:], 0.0)
+        nc.scalar.activation(out=warm2[:], in_=warm[:], func=RELU)
+        make_identity(nc, ident[:])
+
+        weights = {"h": w3, "g": w1, "s": w2}
+        raw = {}
+
+        def load_w(kind, b):
+            for z in range(PASSES):
+                t = keep.tile([P, PACK, P], F32, name=f"raw_{kind}{b}{z}", align_bytes=64)
+                rows = weights[kind][z * P * PACK : (z + 1) * P * PACK, b * P : (b + 1) * P]
+                nc.sync.dma_start(out=t[:], in_=rows.rearrange("(p j) m -> p j m", j=PACK))
+                raw[kind, b, z] = t
+
+        seq = "h0 g0 s0 h1 g1 s1 h2 g2 s2 h3 g3 s3".split()
+        load_w(seq[0][0], int(seq[0][1]))
+        nc.sync.dma_start(out=xw[:], in_=x_words.rearrange("z p c -> p z c"))
+        for q in range(4):
+            nc.sync.dma_start(
+                out=xs[32 * q : 32 * q + 4, :, :].bitcast(I32),
+                in_=x_scales[:, 4 * q : 4 * q + 4, :].rearrange("z q c -> q z c").bitcast(I32),
+            )
+        load_w(seq[1][0], int(seq[1][1]))
+        nc.sync.dma_start(lists[0][:], pos1)
+        load_w(seq[2][0], int(seq[2][1]))
+        nc.sync.dma_start(lists[1][:], pos2)
+        nc.sync.dma_start(lists[2][:], pos3)
+        for x in seq[3:]:
+            load_w(x[0], int(x[1]))
+        alias = {"sc01":"raw_h11","sc02":"raw_g11","sc10":"raw_s11","second0":"raw_h21","sc11":"raw_h21","sc12":"raw_g21","sc20":"raw_s21","second1":"raw_h31","sc21":"raw_h31","sc22":"raw_g31","sc30a":"raw_s31","sc31b":"first3a","sc32b":"second3a"}
+        on_vector = ["h00","g00","g01","s00","s01","h10","h11"]
+
+        res = {}
+        for b in range(BLOCKS):
+            res["h", b] = keep.tile([P, T + SPARE], F32, name=f"h{b}")
+            nc.vector.memset(res["h", b][:, T:], 0.0)
+            res["g", b] = keep.tile([P, T], F32, name=f"g{b}")
+            res["s", b] = keep.tile([P, T], F32, name=f"s{b}")
+
+        grp, accs, banks, sums, scs = {}, {}, {}, {}, {}
+        NA = 2
+        parts = {"": (0, VB), "a": (0, NA), "b": (NA, VB - NA)}
+        halves = [keep.tile([P, n, PACK, P], F32, name=f"yT{u}") for u, n in enumerate((NA, VB - NA))]
+
+        def tile(name):
+            return keep.tile([P, T], F32, name=name, tag=alias.get(name, name), align_bytes=64)
+
+        def cast(x):
+            kind, b = x[0], int(x[1])
+            grouped = keep.tile([P, PASSES, P, PACK], BF16, name=f"grp_{x}", align_bytes=64)
+            grp[x] = grouped
+            for z in range(PASSES):
+                dst = grouped[:, z, :, :].rearrange("p (t q) j -> p q j t", t=PACK)
+                src = raw[kind, b, z][:].rearrange("p j (q t) -> p q j t", t=PACK)
+                if f"{x}{z}" in on_vector:
+                    nc.vector.tensor_copy(out=dst, in_=src)
+                else:
+                    nc.scalar.copy(out=dst, in_=src)
+
+        def quant(x):
+            codes = keep.tile([P, PASSES, P], U32, name=f"cod_{x}", align_bytes=64)
+            scales = keep.tile([P, PASSES, P], U8, name=f"scl_{x}", align_bytes=64)
+            nc.vector.quantize_mx(
+                out=codes[:].rearrange("p z m -> p (z m)").bitcast(FP8X4),
+                scales=scales[:].rearrange("p z m -> p (z m)"),
+                in_=grp[x][:].rearrange("p z m j -> p (z m j)"),
+            )
+            acc = ps_mm.tile([P, T], F32, name="acc", bufs=3)
+            accs[x] = acc
+            for z in range(PASSES):
+                nc.tensor.matmul_mx(
+                    out=acc[:],
+                    lhsT=codes[:, z, :].bitcast(FP8X4),
+                    lhsT_scale=scales[:, z, :],
+                    rhs=xw[:, z, :].bitcast(FP4X4),
+                    rhs_scale=xs[:, z, :],
+                    start=(z == 0),
+                    stop=(z == PASSES - 1),
+                )
+
+        def evac(x):
+            nc.scalar.copy(out=res[x[0], int(x[1])][:, :T], in_=accs[x][:])
+
+        def gather(b, d, p):
+            v0, n = parts[p]
+            scaled = tile(f"sc{b}{d}{p}")
+            scs[b, d, p] = scaled
+            nc.vector.tensor_tensor(
+                scaled[:, : n * P],
+                res["h", b][:].indirect(lists[d][:, v0 * 8 : (v0 + n) * 8]),
+                res["g", b][:, v0 * P : (v0 + n) * P],
+                ALU.mult,
+            )
+
+        def turn(b, d, p):
+            v0, n = parts[p]
+            bank = ps_t.tile([P, VB, P], F32, name="turned")
+            for i in range(n):
+                nc.tensor.matmul(
+                    bank[:, i, :], lhsT=res["s", b][:, (v0 + i) * P : (v0 + i + 1) * P], rhs=ident[:],
+                    start=(i == 0), stop=False, is_transpose=True,
+                )
+            for i in range(n):
+                nc.tensor.matmul(
+                    bank[:, i, :], lhsT=scs[b, d, p][:, i * P : (i + 1) * P], rhs=ident[:],
+                    start=False, stop=(i == n - 1), is_transpose=True,
+                )
+            banks[b, d, p] = bank
+
+        def relu_add(b, d, p):
+            v0, n = parts[p]
+            bank = banks[b, d, p][:, :n, :].rearrange("v i m -> v (i m)")
+            if d == 0:
+                first = tile(f"first{b}{p}")
+                nc.scalar.activation(out=first[:, : n * P], in_=bank, func=RELU)
+                sums[b, p] = first
+            elif d == 1:
+                second = tile(f"second{b}{p}")
+                nc.vector.scalar_tensor_tensor(
+                    out=second[:, : n * P], in0=bank, scalar=0.0, in1=sums[b, p][:, : n * P],
+                    op0=ALU.max, op1=ALU.add,
+                )
+                sums[b, p] = second
+            else:
+                for u, pp in enumerate("ab"):
+                    if p not in ("", pp):
+                        continue
+                    w0, w = parts[pp]
+                    part = slice((w0 - v0) * P, (w0 - v0 + w) * P)
+                    dst = halves[u][:].rearrange("v i t (b q) -> v (i t) b q", q=Q)[:, :, b, :]
+                    nc.vector.scalar_tensor_tensor(
+                        out=dst,
+                        in0=bank[:, part].rearrange("v (r q) -> v r q", q=Q),
+                        scalar=0.0,
+                        in1=sums[b, p][:, part].rearrange("v (r q) -> v r q", q=Q),
+                        op0=ALU.max, op1=ALU.add,
+                    )
+
+        y_codes = keep.tile([P, T], U32, name="y_codes", align_bytes=64)
+        y_scales = keep.tile([P, T], U8, name="y_scales", align_bytes=64)
+        out_rows = out_0.rearrange("(p t) v -> p t v", t=PACK)
+        out_words = out_1[0].rearrange("p c r -> p (c r)").bitcast(I32)
+        styles = "ssmv"
+
+        def finish(vb):
+            cols = slice(vb * P, (vb + 1) * P)
+            u = int(vb >= NA)
+            bank = ps_y.tile([P, PACK, P], F32, name="back")
+            for t in range(PACK):
+                nc.tensor.transpose(bank[:, t, :], halves[u][:, vb - u * NA, t, :], ident[:])
+            rounded = keep.tile([P, P, PACK], BF16, name=f"rounded{vb}", align_bytes=64)
+            y = keep.tile([P, PACK, P], F32, name=f"y{vb}")
+            st = styles[vb]
+            if st == "m":
+                nc.scalar.copy(out=y[:], in_=bank[:])
+                nc.vector.tensor_copy(out=rounded[:], in_=y[:].rearrange("p t v -> p v t"))
+            elif st == "s":
+                nc.scalar.copy(out=rounded[:], in_=bank[:].rearrange("p t v -> p v t"))
+                nc.scalar.copy(out=y[:], in_=bank[:])
+            elif st == "v":
+                nc.vector.tensor_copy(out=y[:], in_=bank[:])
+                nc.vector.tensor_copy(out=rounded[:], in_=y[:].rearrange("p t v -> p v t"))
+            nc.sync.dma_start(out=out_rows[:, :, cols], in_=y[:])
+            nc.vector.quantize_mx(
+                out=y_codes[:, cols].bitcast(FP8X4), scales=y_scales[:, cols],
+                in_=rounded[:].rearrange("p v t -> p (v t)"),
+            )
+            if vb % 2 == 1:
+                both = slice((vb - 1) * P, (vb + 1) * P)
+                nc.scalar.dma_start(out=out_words[:, both], in_=y_codes[:, both].bitcast(I32))
+
+        for w in "ch0 qh0 cg0 cs0 oh0 qg0 ch1 og0 qs0 cg1 os0 G00 qh1 cs1 oh1 T00 A00 G01 qg1 ch2 og1 T01 G02 qs1 cg2 os1 T02 G10 qh2 cs2 oh2 T10 A10 A01 A02 G11 qg2 ch3 og2 T11 G12 qs2 cg3 os2 T12 G20 qh3 cs3 oh3 T20 A20 A11 A12 G21 qg3 og3 T21 G22 qs3 os3 T22 G30a T30a G31a T31a A21 A30a G32a T32a A22 G30b T30b A31a G31b T31b A30b A32a G32b T32b A31b F0 A32b F1 F2 F3".split():
+            k = w[0]
+            if k == "c":
+                cast(w[1:])
+            elif k == "q":
+                quant(w[1:])
+            elif k == "o":
+                evac(w[1:])
+            elif k == "F":
+                finish(int(w[1]))
+            else:
+                {"G": gather, "T": turn, "A": relu_add}[k](int(w[1]), int(w[2]), w[3:])
+        for q in range(4):
+            eng = nc.sync if q % 2 == 0 else nc.scalar
+            eng.dma_start(
+                out=out_2[0, 4 * q : 4 * q + 4, :].bitcast(I32),
+                in_=y_scales[32 * q : 32 * q + 4, :].bitcast(I32),
+            )

@@ -59,7 +59,7 @@ def tile_picked_wfilmg_relu_lo_kernel(
                 nc.sync.dma_start(out=t[:], in_=rows.rearrange("(p j) m -> p j m", j=PACK))
                 raw[kind, b, z] = t
 
-        seq = "h0 g0 s0 h1 g1 s1 h2 g2 s2 h3 g3 s3".split()
+        seq = "h0 g0 h1 s0 g1 s1 h2 g2 s2 h3 g3 s3".split()
         load_w(seq[0][0], int(seq[0][1]))
         nc.sync.dma_start(out=xw[:], in_=x_words.rearrange("z p c -> p z c"))
         for q in range(4):
@@ -74,8 +74,8 @@ def tile_picked_wfilmg_relu_lo_kernel(
         nc.sync.dma_start(lists[2][:], pos3)
         for x in seq[3:]:
             load_w(x[0], int(x[1]))
-        alias = {"sc01":"raw_h11","sc02":"raw_g11","sc10":"raw_s11","second0":"raw_h21","sc11":"raw_h21","sc12":"raw_g21","sc20":"raw_s21","second1":"raw_h31","sc21":"raw_h31","sc22":"raw_g31","sc30a":"raw_s31","sc31b":"first3a","sc32b":"second3a"}
-        on_vector = ["h00","g00","g01","s00","s01","h10","h11"]
+        alias = {"first0":"raw_s10","sc01":"raw_s01","sc02":"raw_s11","first1":"raw_s20","second0":"raw_g20","sc11":"raw_h21","sc12":"raw_s21","first2":"raw_s30","second1":"raw_g30","sc21":"raw_h31","sc22":"raw_s31","sc31b":"first3a","sc32b":"second3a"}
+        on_vector = ["h00","g00","g01","h10","h11"]
 
         res = {}
         for b in range(BLOCKS):
@@ -85,9 +85,9 @@ def tile_picked_wfilmg_relu_lo_kernel(
             res["s", b] = keep.tile([P, T], F32, name=f"s{b}")
 
         grp, accs, banks, sums, scs = {}, {}, {}, {}, {}
-        NA = 2
+        NA = 3
         parts = {"": (0, VB), "a": (0, NA), "b": (NA, VB - NA)}
-        halves = [keep.tile([P, n, PACK, P], F32, name=f"yT{u}") for u, n in enumerate((NA, VB - NA))]
+        halves = [keep.tile([P, PACK, n, P], F32, name=f"yT{u}") for u, n in enumerate((NA, VB - NA))]
 
         def tile(name):
             return keep.tile([P, T], F32, name=name, tag=alias.get(name, name), align_bytes=64)
@@ -97,8 +97,8 @@ def tile_picked_wfilmg_relu_lo_kernel(
             grouped = keep.tile([P, PASSES, P, PACK], BF16, name=f"grp_{x}", align_bytes=64)
             grp[x] = grouped
             for z in range(PASSES):
-                dst = grouped[:, z, :, :].rearrange("p (t q) j -> p q j t", t=PACK)
-                src = raw[kind, b, z][:].rearrange("p j (q t) -> p q j t", t=PACK)
+                dst = grouped[:, z, :, :].rearrange("p (c i) j -> p c j i", i=PACK)
+                src = raw[kind, b, z][:].rearrange("p j (c i) -> p c j i", i=PACK)
                 if f"{x}{z}" in on_vector:
                     nc.vector.tensor_copy(out=dst, in_=src)
                 else:
@@ -156,15 +156,19 @@ def tile_picked_wfilmg_relu_lo_kernel(
 
         def relu_add(b, d, p):
             v0, n = parts[p]
-            bank = banks[b, d, p][:, :n, :].rearrange("v i m -> v (i m)")
+            bank = banks[b, d, p][:, :n, :].rearrange("v i (q t) -> v t i q", t=PACK)
+
+            def dealt(t):
+                return t[:, : n * P].rearrange("v (t i q) -> v t i q", t=PACK, q=Q)
+
             if d == 0:
                 first = tile(f"first{b}{p}")
-                nc.scalar.activation(out=first[:, : n * P], in_=bank, func=RELU)
+                nc.scalar.activation(out=dealt(first), in_=bank, func=RELU)
                 sums[b, p] = first
             elif d == 1:
                 second = tile(f"second{b}{p}")
                 nc.vector.scalar_tensor_tensor(
-                    out=second[:, : n * P], in0=bank, scalar=0.0, in1=sums[b, p][:, : n * P],
+                    out=dealt(second), in0=bank, scalar=0.0, in1=dealt(sums[b, p]),
                     op0=ALU.max, op1=ALU.add,
                 )
                 sums[b, p] = second
@@ -173,13 +177,12 @@ def tile_picked_wfilmg_relu_lo_kernel(
                     if p not in ("", pp):
                         continue
                     w0, w = parts[pp]
-                    part = slice((w0 - v0) * P, (w0 - v0 + w) * P)
-                    dst = halves[u][:].rearrange("v i t (b q) -> v (i t) b q", q=Q)[:, :, b, :]
+                    part = slice(w0 - v0, w0 - v0 + w)
                     nc.vector.scalar_tensor_tensor(
-                        out=dst,
-                        in0=bank[:, part].rearrange("v (r q) -> v r q", q=Q),
+                        out=halves[u][:, :, :, b * Q : (b + 1) * Q],
+                        in0=bank[:, :, part, :],
                         scalar=0.0,
-                        in1=sums[b, p][:, part].rearrange("v (r q) -> v r q", q=Q),
+                        in1=dealt(sums[b, p])[:, :, part, :],
                         op0=ALU.max, op1=ALU.add,
                     )
 
@@ -187,26 +190,35 @@ def tile_picked_wfilmg_relu_lo_kernel(
         y_scales = keep.tile([P, T], U8, name="y_scales", align_bytes=64)
         out_rows = out_0.rearrange("(p t) v -> p t v", t=PACK)
         out_words = out_1[0].rearrange("p c r -> p (c r)").bitcast(I32)
-        styles = "ssmv"
+        styles = "mmmm"
 
         def finish(vb):
             cols = slice(vb * P, (vb + 1) * P)
             u = int(vb >= NA)
-            bank = ps_y.tile([P, PACK, P], F32, name="back")
+            if vb < 2:
+                bank = ps_y.tile([P, PACK, P], F32, name="back")
+            else:
+                bank = ps_mm.tile([P, PACK, P], F32, name="acc", bufs=3)
             for t in range(PACK):
-                nc.tensor.transpose(bank[:, t, :], halves[u][:, vb - u * NA, t, :], ident[:])
+                nc.tensor.transpose(bank[:, t, :], halves[u][:, t, vb - u * NA, :], ident[:])
             rounded = keep.tile([P, P, PACK], BF16, name=f"rounded{vb}", align_bytes=64)
             y = keep.tile([P, PACK, P], F32, name=f"y{vb}")
             st = styles[vb]
             if st == "m":
                 nc.scalar.copy(out=y[:], in_=bank[:])
-                nc.vector.tensor_copy(out=rounded[:], in_=y[:].rearrange("p t v -> p v t"))
+                nc.vector.tensor_copy(
+                    out=rounded[:].rearrange("p (c i) t -> p c t i", i=PACK),
+                    in_=y[:].rearrange("p t (c i) -> p c t i", i=PACK),
+                )
             elif st == "s":
                 nc.scalar.copy(out=rounded[:], in_=bank[:].rearrange("p t v -> p v t"))
                 nc.scalar.copy(out=y[:], in_=bank[:])
             elif st == "v":
                 nc.vector.tensor_copy(out=y[:], in_=bank[:])
-                nc.vector.tensor_copy(out=rounded[:], in_=y[:].rearrange("p t v -> p v t"))
+                nc.vector.tensor_copy(
+                    out=rounded[:].rearrange("p (c i) t -> p c t i", i=PACK),
+                    in_=y[:].rearrange("p t (c i) -> p c t i", i=PACK),
+                )
             nc.sync.dma_start(out=out_rows[:, :, cols], in_=y[:])
             nc.vector.quantize_mx(
                 out=y_codes[:, cols].bitcast(FP8X4), scales=y_scales[:, cols],
@@ -216,7 +228,7 @@ def tile_picked_wfilmg_relu_lo_kernel(
                 both = slice((vb - 1) * P, (vb + 1) * P)
                 nc.scalar.dma_start(out=out_words[:, both], in_=y_codes[:, both].bitcast(I32))
 
-        for w in "ch0 qh0 cg0 cs0 oh0 qg0 ch1 og0 qs0 cg1 os0 G00 qh1 cs1 oh1 T00 A00 G01 qg1 ch2 og1 T01 G02 qs1 cg2 os1 T02 G10 qh2 cs2 oh2 T10 A10 A01 A02 G11 qg2 ch3 og2 T11 G12 qs2 cg3 os2 T12 G20 qh3 cs3 oh3 T20 A20 A11 A12 G21 qg3 og3 T21 G22 qs3 os3 T22 G30a T30a G31a T31a A21 A30a G32a T32a A22 G30b T30b A31a G31b T31b A30b A32a G32b T32b A31b F0 A32b F1 F2 F3".split():
+        for w in "ch0 qh0 cg0 ch1 oh0 qg0 cs0 og0 qh1 cg1 oh1 qs0 cs1 os0 G00 qg1 ch2 og1 T00 A00 G01 qs1 cg2 os1 T01 G02 qh2 cs2 oh2 T02 G10 qg2 ch3 og2 T10 A10 A01 G11 qs2 cg3 os2 T11 G12 qh3 cs3 oh3 T12 A02 G20 qg3 og3 T20 A20 A11 G21 qs3 os3 T21 G22 T22 A12 G30a T30a G31a T31a A21 A30a G32a T32a A22 G30b T30b A31a G31b T31b A30b A32a G32b T32b A31b F0 A32b F1 F2 F3".split():
             k = w[0]
             if k == "c":
                 cast(w[1:])

@@ -15,7 +15,7 @@ U8 = mybir.dt.uint8
 FP8X4 = mybir.dt.float8_e4m3fn_x4
 FP4X4 = mybir.dt.float4_e2m1fn_x4
 ALU = mybir.AluOpType
-RELU = mybir.ActivationFunctionType.Relu
+COPY = mybir.ActivationFunctionType.Copy
 
 P = 128
 PACK = 4
@@ -34,11 +34,11 @@ def tile_picked_wfilmg_relu_lo_kernel(
         keep = ctx.enter_context(tc.tile_pool(name="keep", bufs=1))
         ring = ctx.enter_context(tc.tile_pool(name="ring", bufs=3))
         ps_mm = ctx.enter_context(tc.psum_pool(name="ps_mm", bufs=1))
-        ps_t = ctx.enter_context(tc.psum_pool(name="ps_t", bufs=3))
+        ps_t = ctx.enter_context(tc.psum_pool(name="ps_t", bufs=2))
         ps_y = ctx.enter_context(tc.psum_pool(name="ps_y", bufs=2))
 
         lists = [keep.tile([P, T // 16], U16, name=f"list{d}") for d in range(3)]
-        xw = keep.tile([P, PASSES, 2 * T], U8, name="xw", align_bytes=64)
+        xw = [keep.tile([P, 2 * T], U8, name=f"xw{z}", align_bytes=64) for z in range(PASSES)]
         xs = keep.tile([P, PASSES, T], U8, name="xs", align_bytes=64)
         ident = keep.tile([P, P], F32, name="ident")
         warm = keep.tile([P, 8], F32, name="warm")
@@ -46,7 +46,7 @@ def tile_picked_wfilmg_relu_lo_kernel(
 
         nc.vector.memset(xs[:].rearrange("p z c -> p (z c)").bitcast(I32), 0)
         nc.vector.memset(warm[:], 0.0)
-        nc.scalar.activation(out=warm2[:], in_=warm[:], func=RELU)
+        nc.scalar.activation(out=warm2[:], in_=warm[:], func=COPY, scale=3.0)
         make_identity(nc, ident[:])
 
         weights = {"h": w3, "g": w1, "s": w2}
@@ -59,23 +59,24 @@ def tile_picked_wfilmg_relu_lo_kernel(
                 nc.sync.dma_start(out=t[:], in_=rows.rearrange("(p j) m -> p j m", j=PACK))
                 raw[kind, b, z] = t
 
-        seq = "h0 g0 h1 s0 g1 s1 h2 g2 s2 h3 g3 s3".split()
+        seq = "h0 g0 s0 h1 g1 s1 h2 g2 s2 h3 g3 s3".split()
         load_w(seq[0][0], int(seq[0][1]))
-        nc.sync.dma_start(out=xw[:], in_=x_words.rearrange("z p c -> p z c"))
+        nc.sync.dma_start(out=xw[0][:], in_=x_words[0])
         for q in range(4):
             nc.sync.dma_start(
                 out=xs[32 * q : 32 * q + 4, :, :].bitcast(I32),
                 in_=x_scales[:, 4 * q : 4 * q + 4, :].rearrange("z q c -> q z c").bitcast(I32),
             )
         load_w(seq[1][0], int(seq[1][1]))
+        nc.sync.dma_start(out=xw[1][:], in_=x_words[1])
         nc.sync.dma_start(lists[0][:], pos1)
         load_w(seq[2][0], int(seq[2][1]))
         nc.sync.dma_start(lists[1][:], pos2)
         nc.sync.dma_start(lists[2][:], pos3)
         for x in seq[3:]:
             load_w(x[0], int(x[1]))
-        alias = {"first0":"raw_s10","sc01":"raw_s01","sc02":"raw_s11","first1":"raw_s20","second0":"raw_g20","sc11":"raw_h21","sc12":"raw_s21","first2":"raw_s30","second1":"raw_g30","sc21":"raw_h31","sc22":"raw_s31","sc31b":"first3a","sc32b":"second3a"}
-        on_vector = ["h00","g00","g01","h10","h11"]
+        alias = {"sc00":"raw_s01","sc01":"raw_h11","sc02":"raw_g11","sc10":"raw_s11","sc11":"raw_h21","sc12":"raw_g21","sc20":"raw_s21","sc21":"raw_h31","sc22":"raw_g31"}
+        on_vector = ["h00","g00","g01","s00","s01"]
 
         res = {}
         for b in range(BLOCKS):
@@ -85,7 +86,7 @@ def tile_picked_wfilmg_relu_lo_kernel(
             res["s", b] = keep.tile([P, T], F32, name=f"s{b}")
 
         grp, accs, banks, sums, scs = {}, {}, {}, {}, {}
-        NA = 3
+        NA = 2
         parts = {"": (0, VB), "a": (0, NA), "b": (NA, VB - NA)}
         halves = [keep.tile([P, PACK, n, P], F32, name=f"yT{u}") for u, n in enumerate((NA, VB - NA))]
 
@@ -107,26 +108,37 @@ def tile_picked_wfilmg_relu_lo_kernel(
         def quant(x):
             codes = keep.tile([P, PASSES, P], U32, name=f"cod_{x}", align_bytes=64)
             scales = keep.tile([P, PASSES, P], U8, name=f"scl_{x}", align_bytes=64)
-            nc.vector.quantize_mx(
-                out=codes[:].rearrange("p z m -> p (z m)").bitcast(FP8X4),
-                scales=scales[:].rearrange("p z m -> p (z m)"),
-                in_=grp[x][:].rearrange("p z m j -> p (z m j)"),
-            )
-            acc = ps_mm.tile([P, T], F32, name="acc", bufs=3)
+            if x in seq[:2]:
+                for z in range(PASSES):
+                    nc.vector.quantize_mx(
+                        out=codes[:, z, :].bitcast(FP8X4),
+                        scales=scales[:, z, :],
+                        in_=grp[x][:, z, :, :].rearrange("p m j -> p (m j)"),
+                    )
+            else:
+                nc.vector.quantize_mx(
+                    out=codes[:].rearrange("p z m -> p (z m)").bitcast(FP8X4),
+                    scales=scales[:].rearrange("p z m -> p (z m)"),
+                    in_=grp[x][:].rearrange("p z m j -> p (z m j)"),
+                )
+            acc = ps_mm.tile([P, T], F32, name="accs" if x[0] == "s" else "acc", bufs=2)
             accs[x] = acc
             for z in range(PASSES):
                 nc.tensor.matmul_mx(
                     out=acc[:],
                     lhsT=codes[:, z, :].bitcast(FP8X4),
                     lhsT_scale=scales[:, z, :],
-                    rhs=xw[:, z, :].bitcast(FP4X4),
+                    rhs=xw[z][:].bitcast(FP4X4),
                     rhs_scale=xs[:, z, :],
                     start=(z == 0),
                     stop=(z == PASSES - 1),
                 )
 
         def evac(x):
-            nc.scalar.copy(out=res[x[0], int(x[1])][:, :T], in_=accs[x][:])
+            if x[0] == "s":
+                nc.scalar.activation(out=res["s", int(x[1])][:], in_=accs[x][:], func=COPY, scale=3.0)
+            else:
+                nc.scalar.copy(out=res[x[0], int(x[1])][:, :T], in_=accs[x][:])
 
         def gather(b, d, p):
             v0, n = parts[p]
@@ -139,52 +151,40 @@ def tile_picked_wfilmg_relu_lo_kernel(
                 ALU.mult,
             )
 
+        def floor_at(b, d, p):
+            v0, n = parts[p]
+            m = tile(f"m{b}{d}{p}")
+            sums[b, d, p] = m
+            nc.vector.scalar_tensor_tensor(
+                out=m[:, : n * P], in0=accs[f"s{b}"][:, v0 * P : (v0 + n) * P], scalar=-1.0,
+                in1=scs[b, d, p][:, : n * P], op0=ALU.mult, op1=ALU.max,
+            )
+
         def turn(b, d, p):
             v0, n = parts[p]
-            bank = ps_t.tile([P, VB, P], F32, name="turned")
-            for i in range(n):
-                nc.tensor.matmul(
-                    bank[:, i, :], lhsT=res["s", b][:, (v0 + i) * P : (v0 + i + 1) * P], rhs=ident[:],
-                    start=(i == 0), stop=False, is_transpose=True,
-                )
-            for i in range(n):
-                nc.tensor.matmul(
-                    bank[:, i, :], lhsT=scs[b, d, p][:, i * P : (i + 1) * P], rhs=ident[:],
-                    start=False, stop=(i == n - 1), is_transpose=True,
-                )
-            banks[b, d, p] = bank
-
-        def relu_add(b, d, p):
-            v0, n = parts[p]
-            bank = banks[b, d, p][:, :n, :].rearrange("v i (q t) -> v t i q", t=PACK)
-
-            def dealt(t):
-                return t[:, : n * P].rearrange("v (t i q) -> v t i q", t=PACK, q=Q)
-
             if d == 0:
-                first = tile(f"first{b}{p}")
-                nc.scalar.activation(out=dealt(first), in_=bank, func=RELU)
-                sums[b, p] = first
-            elif d == 1:
-                second = tile(f"second{b}{p}")
-                nc.vector.scalar_tensor_tensor(
-                    out=dealt(second), in0=bank, scalar=0.0, in1=dealt(sums[b, p]),
-                    op0=ALU.max, op1=ALU.add,
+                banks[b, p] = ps_t.tile([P, VB, P], F32, name="turned")
+            bank = banks[b, p]
+            for i in range(n):
+                nc.tensor.matmul(
+                    bank[:, i, :], lhsT=sums[b, d, p][:, i * P : (i + 1) * P], rhs=ident[:],
+                    start=(i == 0 and d == 0), stop=False, is_transpose=True,
                 )
-                sums[b, p] = second
-            else:
-                for u, pp in enumerate("ab"):
-                    if p not in ("", pp):
-                        continue
-                    w0, w = parts[pp]
-                    part = slice(w0 - v0, w0 - v0 + w)
-                    nc.vector.scalar_tensor_tensor(
-                        out=halves[u][:, :, :, b * Q : (b + 1) * Q],
-                        in0=bank[:, :, part, :],
-                        scalar=0.0,
-                        in1=dealt(sums[b, p])[:, :, part, :],
-                        op0=ALU.max, op1=ALU.add,
+            if d == 2:
+                for i in range(n):
+                    nc.tensor.matmul(
+                        bank[:, i, :], lhsT=res["s", b][:, (v0 + i) * P : (v0 + i + 1) * P], rhs=ident[:],
+                        start=False, stop=(i == n - 1), is_transpose=True,
                     )
+
+        def deal(b, d, p):
+            v0, n = parts[p]
+            bank = banks[b, p][:, :n, :].rearrange("v i (q t) -> v t i q", t=PACK)
+            for u, pp in enumerate("ab"):
+                if p not in ("", pp):
+                    continue
+                w0, w = parts[pp]
+                nc.scalar.copy(out=halves[u][:, :, :, b * Q : (b + 1) * Q], in_=bank[:, :, w0 - v0 : w0 - v0 + w, :])
 
         y_codes = keep.tile([P, T], U32, name="y_codes", align_bytes=64)
         y_scales = keep.tile([P, T], U8, name="y_scales", align_bytes=64)
@@ -198,7 +198,7 @@ def tile_picked_wfilmg_relu_lo_kernel(
             if vb < 2:
                 bank = ps_y.tile([P, PACK, P], F32, name="back")
             else:
-                bank = ps_mm.tile([P, PACK, P], F32, name="acc", bufs=3)
+                bank = ps_mm.tile([P, PACK, P], F32, name="acc", bufs=2)
             for t in range(PACK):
                 nc.tensor.transpose(bank[:, t, :], halves[u][:, t, vb - u * NA, :], ident[:])
             rounded = keep.tile([P, P, PACK], BF16, name=f"rounded{vb}", align_bytes=64)
@@ -228,7 +228,7 @@ def tile_picked_wfilmg_relu_lo_kernel(
                 both = slice((vb - 1) * P, (vb + 1) * P)
                 nc.scalar.dma_start(out=out_words[:, both], in_=y_codes[:, both].bitcast(I32))
 
-        for w in "ch0 qh0 cg0 ch1 oh0 qg0 cs0 og0 qh1 cg1 oh1 qs0 cs1 os0 G00 qg1 ch2 og1 T00 A00 G01 qs1 cg2 os1 T01 G02 qh2 cs2 oh2 T02 G10 qg2 ch3 og2 T10 A10 A01 G11 qs2 cg3 os2 T11 G12 qh3 cs3 oh3 T12 A02 G20 qg3 og3 T20 A20 A11 G21 qs3 os3 T21 G22 T22 A12 G30a T30a G31a T31a A21 A30a G32a T32a A22 G30b T30b A31a G31b T31b A30b A32a G32b T32b A31b F0 A32b F1 F2 F3".split():
+        for w in "ch0 qh0 cg0 cs0 oh0 qg0 ch1 og0 qs0 cg1 os0 G00 qh1 cs1 oh1 G01 qg1 ch2 og1 M00 U00 G02 qs1 cg2 os1 M01 U01 M02 U02 E00 G10 qh2 cs2 oh2 G11 qg2 ch3 og2 M10 U10 G12 qs2 cg3 os2 M11 U11 M12 U12 E10 G20 qh3 cs3 oh3 G21 qg3 og3 M20 U20 G22 qs3 os3 M21 U21 M22 U22 E20 G30a G31a M30a U30a G32a M31a U31a G30b M32a U32a E30a G31b M30b U30b G32b M31b U31b M32b U32b F0 E30b F1 F2 F3".split():
             k = w[0]
             if k == "c":
                 cast(w[1:])
@@ -239,7 +239,7 @@ def tile_picked_wfilmg_relu_lo_kernel(
             elif k == "F":
                 finish(int(w[1]))
             else:
-                {"G": gather, "T": turn, "A": relu_add}[k](int(w[1]), int(w[2]), w[3:])
+                {"G": gather, "U": turn, "M": floor_at, "E": deal}[k](int(w[1]), int(w[2]), w[3:])
         for q in range(4):
             eng = nc.sync if q % 2 == 0 else nc.scalar
             eng.dma_start(

@@ -21,9 +21,11 @@ P = 128
 PACK = 4
 PASSES = K // (P * PACK)
 BLOCKS = N // P
-VB = T // P
+CHUNKS = T // P
+LISTS = 3
 SPARE = 16
 Q = P // PACK
+LAST = BLOCKS - 1
 
 
 def tile_picked_wfilmg_relu_lo_kernel(
@@ -32,12 +34,9 @@ def tile_picked_wfilmg_relu_lo_kernel(
     nc = tc.nc
     with ExitStack() as ctx:
         keep = ctx.enter_context(tc.tile_pool(name="keep", bufs=1))
-        ring = ctx.enter_context(tc.tile_pool(name="ring", bufs=3))
-        ps_mm = ctx.enter_context(tc.psum_pool(name="ps_mm", bufs=1))
-        ps_t = ctx.enter_context(tc.psum_pool(name="ps_t", bufs=2))
-        ps_y = ctx.enter_context(tc.psum_pool(name="ps_y", bufs=2))
+        psum = ctx.enter_context(tc.psum_pool(name="psum", bufs=2))
 
-        lists = [keep.tile([P, T // 16], U16, name=f"list{d}") for d in range(3)]
+        lists = [keep.tile([P, T // 16], U16, name=f"list{d}") for d in range(LISTS)]
         xw = [keep.tile([P, 2 * T], U8, name=f"xw{z}", align_bytes=64) for z in range(PASSES)]
         xs = keep.tile([P, PASSES, T], U8, name="xs", align_bytes=64)
         ident = keep.tile([P, P], F32, name="ident")
@@ -50,6 +49,7 @@ def tile_picked_wfilmg_relu_lo_kernel(
         make_identity(nc, ident[:])
 
         weights = {"h": w3, "g": w1, "s": w2}
+        products = [(kind, b) for b in range(BLOCKS) for kind in "hgs"]
         raw = {}
 
         def load_w(kind, b):
@@ -59,24 +59,22 @@ def tile_picked_wfilmg_relu_lo_kernel(
                 nc.sync.dma_start(out=t[:], in_=rows.rearrange("(p j) m -> p j m", j=PACK))
                 raw[kind, b, z] = t
 
-        seq = "h0 g0 s0 h1 g1 s1 h2 g2 s2 h3 g3 s3".split()
-        load_w(seq[0][0], int(seq[0][1]))
+        load_w("h", 0)
         nc.sync.dma_start(out=xw[0][:], in_=x_words[0])
         for q in range(4):
             nc.sync.dma_start(
                 out=xs[32 * q : 32 * q + 4, :, :].bitcast(I32),
                 in_=x_scales[:, 4 * q : 4 * q + 4, :].rearrange("z q c -> q z c").bitcast(I32),
             )
-        load_w(seq[1][0], int(seq[1][1]))
+        load_w("g", 0)
         nc.sync.dma_start(out=xw[1][:], in_=x_words[1])
         nc.sync.dma_start(lists[0][:], pos1)
-        load_w(seq[2][0], int(seq[2][1]))
+        load_w("s", 0)
         nc.sync.dma_start(lists[1][:], pos2)
         nc.sync.dma_start(lists[2][:], pos3)
-        for x in seq[3:]:
-            load_w(x[0], int(x[1]))
-        alias = {"sc00":"raw_s01","sc01":"raw_h11","sc02":"raw_g11","sc10":"raw_s11","sc11":"raw_h21","sc12":"raw_g21","sc20":"raw_s21","sc21":"raw_h31","sc22":"raw_g31"}
-        on_vector = ["h00","g00","g01","s00","s01"]
+        for kind, b in products[3:]:
+            load_w(kind, b)
+        on_vector = [("h", 0, 0), ("g", 0, 0), ("g", 0, 1), ("s", 0, 0), ("s", 0, 1)]
 
         res = {}
         for b in range(BLOCKS):
@@ -85,44 +83,42 @@ def tile_picked_wfilmg_relu_lo_kernel(
             res["g", b] = keep.tile([P, T], F32, name=f"g{b}")
             res["s", b] = keep.tile([P, T], F32, name=f"s{b}")
 
-        grp, accs, banks, sums, scs = {}, {}, {}, {}, {}
-        NA = 2
-        parts = {"": (0, VB), "a": (0, NA), "b": (NA, VB - NA)}
-        halves = [keep.tile([P, PACK, n, P], F32, name=f"yT{u}") for u, n in enumerate((NA, VB - NA))]
+        grp, accs, banks, tops, scaled = {}, {}, {}, {}, {}
+        turned = keep.tile([P, CHUNKS, PACK, P], F32, name="turned")
 
-        def tile(name):
-            return keep.tile([P, T], F32, name=name, tag=alias.get(name, name), align_bytes=64)
-
-        def cast(x):
-            kind, b = x[0], int(x[1])
-            grouped = keep.tile([P, PASSES, P, PACK], BF16, name=f"grp_{x}", align_bytes=64)
-            grp[x] = grouped
+        def cast(i):
+            if i >= len(products):
+                return
+            kind, b = products[i]
+            grouped = keep.tile([P, PASSES, P, PACK], BF16, name=f"grp_{kind}{b}", align_bytes=64)
+            grp[i] = grouped
             for z in range(PASSES):
                 dst = grouped[:, z, :, :].rearrange("p (c i) j -> p c j i", i=PACK)
                 src = raw[kind, b, z][:].rearrange("p j (c i) -> p c j i", i=PACK)
-                if f"{x}{z}" in on_vector:
+                if (kind, b, z) in on_vector:
                     nc.vector.tensor_copy(out=dst, in_=src)
                 else:
                     nc.scalar.copy(out=dst, in_=src)
 
-        def quant(x):
-            codes = keep.tile([P, PASSES, P], U32, name=f"cod_{x}", align_bytes=64)
-            scales = keep.tile([P, PASSES, P], U8, name=f"scl_{x}", align_bytes=64)
-            if x in seq[:2]:
+        def multiply(i):
+            kind, b = products[i]
+            codes = keep.tile([P, PASSES, P], U32, name=f"cod_{kind}{b}", align_bytes=64)
+            scales = keep.tile([P, PASSES, P], U8, name=f"scl_{kind}{b}", align_bytes=64)
+            if i < 2:
                 for z in range(PASSES):
                     nc.vector.quantize_mx(
                         out=codes[:, z, :].bitcast(FP8X4),
                         scales=scales[:, z, :],
-                        in_=grp[x][:, z, :, :].rearrange("p m j -> p (m j)"),
+                        in_=grp[i][:, z, :, :].rearrange("p m j -> p (m j)"),
                     )
             else:
                 nc.vector.quantize_mx(
                     out=codes[:].rearrange("p z m -> p (z m)").bitcast(FP8X4),
                     scales=scales[:].rearrange("p z m -> p (z m)"),
-                    in_=grp[x][:].rearrange("p z m j -> p (z m j)"),
+                    in_=grp[i][:].rearrange("p z m j -> p (z m j)"),
                 )
-            acc = ps_mm.tile([P, T], F32, name="accs" if x[0] == "s" else "acc", bufs=2)
-            accs[x] = acc
+            acc = psum.tile([P, T], F32, name="shift" if kind == "s" else "acc")
+            accs[kind, b] = acc
             for z in range(PASSES):
                 nc.tensor.matmul_mx(
                     out=acc[:],
@@ -134,112 +130,127 @@ def tile_picked_wfilmg_relu_lo_kernel(
                     stop=(z == PASSES - 1),
                 )
 
-        def evac(x):
-            if x[0] == "s":
-                nc.scalar.activation(out=res["s", int(x[1])][:], in_=accs[x][:], func=COPY, scale=3.0)
+        def empty(i):
+            kind, b = products[i]
+            if kind == "s":
+                nc.scalar.activation(out=res["s", b][:], in_=accs[kind, b][:], func=COPY, scale=float(LISTS))
             else:
-                nc.scalar.copy(out=res[x[0], int(x[1])][:, :T], in_=accs[x][:])
+                nc.scalar.copy(out=res[kind, b][:, :T], in_=accs[kind, b][:])
 
-        def gather(b, d, p):
-            v0, n = parts[p]
-            scaled = tile(f"sc{b}{d}{p}")
-            scs[b, d, p] = scaled
+        def gather(b, d, v0, n, tag):
+            a = keep.tile([P, T], F32, name=f"a{b}{d}{v0}", tag=tag, align_bytes=64)
+            scaled[b, d, v0] = a
             nc.vector.tensor_tensor(
-                scaled[:, : n * P],
+                a[:, : n * P],
                 res["h", b][:].indirect(lists[d][:, v0 * 8 : (v0 + n) * 8]),
                 res["g", b][:, v0 * P : (v0 + n) * P],
                 ALU.mult,
             )
 
-        def floor_at(b, d, p):
-            v0, n = parts[p]
-            m = tile(f"m{b}{d}{p}")
-            sums[b, d, p] = m
+        def floor_at(b, d, v0, n):
+            m = keep.tile([P, n * P], F32, name=f"m{b}{d}{v0}", align_bytes=64)
+            tops[b, d, v0] = m
             nc.vector.scalar_tensor_tensor(
-                out=m[:, : n * P], in0=accs[f"s{b}"][:, v0 * P : (v0 + n) * P], scalar=-1.0,
-                in1=scs[b, d, p][:, : n * P], op0=ALU.mult, op1=ALU.max,
+                out=m[:], in0=accs["s", b][:, v0 * P : (v0 + n) * P], scalar=-1.0,
+                in1=scaled[b, d, v0][:, : n * P], op0=ALU.mult, op1=ALU.max,
             )
 
-        def turn(b, d, p):
-            v0, n = parts[p]
-            if d == 0:
-                banks[b, p] = ps_t.tile([P, VB, P], F32, name="turned")
-            bank = banks[b, p]
+        def open_sum(b, v0, n):
+            bank = psum.tile([P, CHUNKS, P], F32, name="sum")
+            banks[b, v0] = bank
             for i in range(n):
                 nc.tensor.matmul(
-                    bank[:, i, :], lhsT=sums[b, d, p][:, i * P : (i + 1) * P], rhs=ident[:],
-                    start=(i == 0 and d == 0), stop=False, is_transpose=True,
+                    bank[:, i, :], lhsT=res["s", b][:, (v0 + i) * P : (v0 + i + 1) * P], rhs=ident[:],
+                    start=(i == 0), stop=False, is_transpose=True,
                 )
-            if d == 2:
-                for i in range(n):
-                    nc.tensor.matmul(
-                        bank[:, i, :], lhsT=res["s", b][:, (v0 + i) * P : (v0 + i + 1) * P], rhs=ident[:],
-                        start=False, stop=(i == n - 1), is_transpose=True,
-                    )
 
-        def deal(b, d, p):
-            v0, n = parts[p]
-            bank = banks[b, p][:, :n, :].rearrange("v i (q t) -> v t i q", t=PACK)
-            for u, pp in enumerate("ab"):
-                if p not in ("", pp):
-                    continue
-                w0, w = parts[pp]
-                nc.scalar.copy(out=halves[u][:, :, :, b * Q : (b + 1) * Q], in_=bank[:, :, w0 - v0 : w0 - v0 + w, :])
+        def add_to_sum(b, d, v0, n):
+            for i in range(n):
+                nc.tensor.matmul(
+                    banks[b, v0][:, i, :], lhsT=tops[b, d, v0][:, i * P : (i + 1) * P], rhs=ident[:],
+                    start=False, stop=(d == LISTS - 1 and i == n - 1), is_transpose=True,
+                )
+
+        def deal(b, v0, n):
+            nc.scalar.copy(
+                out=turned[:, v0 : v0 + n, :, b * Q : (b + 1) * Q],
+                in_=banks[b, v0][:, :n, :].rearrange("v i (q t) -> v i t q", t=PACK),
+            )
 
         y_codes = keep.tile([P, T], U32, name="y_codes", align_bytes=64)
         y_scales = keep.tile([P, T], U8, name="y_scales", align_bytes=64)
         out_rows = out_0.rearrange("(p t) v -> p t v", t=PACK)
         out_words = out_1[0].rearrange("p c r -> p (c r)").bitcast(I32)
-        styles = "mmmm"
+        ys = {}
 
-        def finish(vb):
-            cols = slice(vb * P, (vb + 1) * P)
-            u = int(vb >= NA)
-            if vb < 2:
-                bank = ps_y.tile([P, PACK, P], F32, name="back")
-            else:
-                bank = ps_mm.tile([P, PACK, P], F32, name="acc", bufs=2)
+        def turn_back(i):
+            bank = psum.tile([P, PACK, P], F32, name="back")
             for t in range(PACK):
-                nc.tensor.transpose(bank[:, t, :], halves[u][:, t, vb - u * NA, :], ident[:])
-            rounded = keep.tile([P, P, PACK], BF16, name=f"rounded{vb}", align_bytes=64)
-            y = keep.tile([P, PACK, P], F32, name=f"y{vb}")
-            st = styles[vb]
-            if st == "m":
-                nc.scalar.copy(out=y[:], in_=bank[:])
-                nc.vector.tensor_copy(
-                    out=rounded[:].rearrange("p (c i) t -> p c t i", i=PACK),
-                    in_=y[:].rearrange("p t (c i) -> p c t i", i=PACK),
-                )
-            elif st == "s":
-                nc.scalar.copy(out=rounded[:], in_=bank[:].rearrange("p t v -> p v t"))
-                nc.scalar.copy(out=y[:], in_=bank[:])
-            elif st == "v":
-                nc.vector.tensor_copy(out=y[:], in_=bank[:])
-                nc.vector.tensor_copy(
-                    out=rounded[:].rearrange("p (c i) t -> p c t i", i=PACK),
-                    in_=y[:].rearrange("p t (c i) -> p c t i", i=PACK),
-                )
-            nc.sync.dma_start(out=out_rows[:, :, cols], in_=y[:])
+                nc.tensor.transpose(bank[:, t, :], turned[:, i, t, :], ident[:])
+            y = keep.tile([P, PACK, P], F32, name=f"y{i}")
+            ys[i] = y
+            nc.scalar.copy(out=y[:], in_=bank[:])
+            nc.sync.dma_start(out=out_rows[:, :, i * P : (i + 1) * P], in_=y[:])
+
+        def round_y(i):
+            nc.vector.tensor_copy(
+                out=rounded[:, i * P : (i + 1) * P, :].rearrange("p (c i) t -> p c t i", i=PACK),
+                in_=ys[i][:].rearrange("p t (c i) -> p c t i", i=PACK),
+            )
+
+        def quantize_y(i, n):
+            cols = slice(i * P, (i + n) * P)
             nc.vector.quantize_mx(
                 out=y_codes[:, cols].bitcast(FP8X4), scales=y_scales[:, cols],
-                in_=rounded[:].rearrange("p v t -> p (v t)"),
+                in_=rounded[:, cols, :].rearrange("p v t -> p (v t)"),
             )
-            if vb % 2 == 1:
-                both = slice((vb - 1) * P, (vb + 1) * P)
-                nc.scalar.dma_start(out=out_words[:, both], in_=y_codes[:, both].bitcast(I32))
 
-        for w in "ch0 qh0 cg0 cs0 oh0 qg0 ch1 og0 qs0 cg1 os0 G00 qh1 cs1 oh1 G01 qg1 ch2 og1 M00 U00 G02 qs1 cg2 os1 M01 U01 M02 U02 E00 G10 qh2 cs2 oh2 G11 qg2 ch3 og2 M10 U10 G12 qs2 cg3 os2 M11 U11 M12 U12 E10 G20 qh3 cs3 oh3 G21 qg3 og3 M20 U20 G22 qs3 os3 M21 U21 M22 U22 E20 G30a G31a M30a U30a G32a M31a U31a G30b M32a U32a E30a G31b M30b U30b G32b M31b U31b M32b U32b F0 E30b F1 F2 F3".split():
-            k = w[0]
-            if k == "c":
-                cast(w[1:])
-            elif k == "q":
-                quant(w[1:])
-            elif k == "o":
-                evac(w[1:])
-            elif k == "F":
-                finish(int(w[1]))
-            else:
-                {"G": gather, "U": turn, "M": floor_at, "E": deal}[k](int(w[1]), int(w[2]), w[3:])
+        cast(0)
+        multiply(0)
+        cast(1)
+        cast(2)
+        empty(0)
+        multiply(1)
+        cast(3)
+        empty(1)
+        multiply(2)
+        cast(4)
+        empty(2)
+        for b in range(LAST):
+            for d in range(LISTS):
+                i = LISTS * (b + 1) + d
+                kind, kb = products[i - 1]
+                gather(b, d, 0, CHUNKS, f"raw_{kind}{kb}1")
+                if d == 2:
+                    open_sum(b, 0, CHUNKS)
+                    floor_at(b, 0, 0, CHUNKS)
+                    add_to_sum(b, 0, 0, CHUNKS)
+                multiply(i)
+                cast(i + 2)
+                empty(i)
+            for d in (1, 2):
+                floor_at(b, d, 0, CHUNKS)
+                add_to_sum(b, d, 0, CHUNKS)
+            deal(b, 0, CHUNKS)
+        for i in range(CHUNKS):
+            for d in range(LISTS):
+                gather(LAST, d, i, 1, f"a{d}")
+            open_sum(LAST, i, 1)
+            for d in range(LISTS):
+                floor_at(LAST, d, i, 1)
+                add_to_sum(LAST, d, i, 1)
+            deal(LAST, i, 1)
+            turn_back(i)
+        rounded = keep.tile([P, T, PACK], BF16, name="rounded", tag="a2", align_bytes=64)
+        round_y(0)
+        round_y(1)
+        round_y(2)
+        quantize_y(0, 2)
+        nc.scalar.dma_start(out=out_words[:, : 2 * P], in_=y_codes[:, : 2 * P].bitcast(I32))
+        quantize_y(2, 1)
+        round_y(3)
+        quantize_y(3, 1)
+        nc.sync.dma_start(out=out_words[:, 2 * P :], in_=y_codes[:, 2 * P :].bitcast(I32))
         for q in range(4):
             eng = nc.sync if q % 2 == 0 else nc.scalar
             eng.dma_start(

@@ -23,7 +23,7 @@ PASSES = K // (P * PACK)
 BLOCKS = N // P
 CHUNKS = T // P
 LISTS = 3
-SPARE = 16
+SPARE = 192
 Q = P // PACK
 LAST = BLOCKS - 1
 
@@ -37,8 +37,9 @@ def tile_picked_wfilmg_relu_lo_kernel(
         psum = ctx.enter_context(tc.psum_pool(name="psum", bufs=2))
 
         lists = [keep.tile([P, T // 16], U16, name=f"list{d}") for d in range(LISTS)]
-        xw = [keep.tile([P, 2 * T], U8, name=f"xw{z}", align_bytes=64) for z in range(PASSES)]
+        xw = keep.tile([P, PASSES, 2 * T], U8, name="xw", align_bytes=64)
         xs = keep.tile([P, PASSES, T], U8, name="xs", align_bytes=64)
+        xs_in = keep.tile([P, PASSES, T], U8, name="xs_in", align_bytes=64)
         ident = keep.tile([P, P], F32, name="ident")
         warm = keep.tile([P, 8], F32, name="warm")
         warm2 = keep.tile([P, 8], F32, name="warm2")
@@ -59,22 +60,26 @@ def tile_picked_wfilmg_relu_lo_kernel(
                 nc.sync.dma_start(out=t[:], in_=rows.rearrange("(p j) m -> p j m", j=PACK))
                 raw[kind, b, z] = t
 
-        load_w("h", 0)
-        nc.sync.dma_start(out=xw[0][:], in_=x_words[0])
         for q in range(4):
             nc.sync.dma_start(
-                out=xs[32 * q : 32 * q + 4, :, :].bitcast(I32),
+                out=xs_in[32 * q : 32 * q + 4, :, :].bitcast(I32),
                 in_=x_scales[:, 4 * q : 4 * q + 4, :].rearrange("z q c -> q z c").bitcast(I32),
             )
+        load_w("h", 0)
+        nc.sync.dma_start(out=xw[:], in_=x_words.rearrange("z p c -> p z c"))
         load_w("g", 0)
-        nc.sync.dma_start(out=xw[1][:], in_=x_words[1])
         nc.sync.dma_start(lists[0][:], pos1)
         load_w("s", 0)
         nc.sync.dma_start(lists[1][:], pos2)
+        load_w("h", 1)
         nc.sync.dma_start(lists[2][:], pos3)
-        for kind, b in products[3:]:
+        for kind, b in products[4:]:
             load_w(kind, b)
-        on_vector = [("h", 0, 0), ("g", 0, 0), ("g", 0, 1), ("s", 0, 0), ("s", 0, 1)]
+        for q in range(4):
+            nc.vector.tensor_copy(
+                out=xs[32 * q : 32 * q + 4, :, :].bitcast(I32), in_=xs_in[32 * q : 32 * q + 4, :, :].bitcast(I32)
+            )
+        on_vector = [("h", 0, 1), ("g", 0, 1)]
 
         res = {}
         for b in range(BLOCKS):
@@ -84,13 +89,12 @@ def tile_picked_wfilmg_relu_lo_kernel(
             res["s", b] = keep.tile([P, T], F32, name=f"s{b}")
 
         grp, accs, banks, tops, scaled = {}, {}, {}, {}, {}
-        turned = keep.tile([P, CHUNKS, PACK, P], F32, name="turned")
 
         def cast(i):
             if i >= len(products):
                 return
             kind, b = products[i]
-            grouped = keep.tile([P, PASSES, P, PACK], BF16, name=f"grp_{kind}{b}", align_bytes=64)
+            grouped = keep.tile([P, PASSES, P, PACK], BF16, name=f"grp{i}", tag="cod1" if i == 3 else f"grp{i}", align_bytes=64)
             grp[i] = grouped
             for z in range(PASSES):
                 dst = grouped[:, z, :, :].rearrange("p (c i) j -> p c j i", i=PACK)
@@ -102,7 +106,7 @@ def tile_picked_wfilmg_relu_lo_kernel(
 
         def multiply(i):
             kind, b = products[i]
-            codes = keep.tile([P, PASSES, P], U32, name=f"cod_{kind}{b}", align_bytes=64)
+            codes = keep.tile([P, PASSES, P], U32, name=f"cod{i}", tag=f"cod{i}", align_bytes=64)
             scales = keep.tile([P, PASSES, P], U8, name=f"scl_{kind}{b}", align_bytes=64)
             if i < 2:
                 for z in range(PASSES):
@@ -124,7 +128,7 @@ def tile_picked_wfilmg_relu_lo_kernel(
                     out=acc[:],
                     lhsT=codes[:, z, :].bitcast(FP8X4),
                     lhsT_scale=scales[:, z, :],
-                    rhs=xw[z][:].bitcast(FP4X4),
+                    rhs=xw[:, z, :].bitcast(FP4X4),
                     rhs_scale=xs[:, z, :],
                     start=(z == 0),
                     stop=(z == PASSES - 1),
@@ -147,8 +151,8 @@ def tile_picked_wfilmg_relu_lo_kernel(
                 ALU.mult,
             )
 
-        def floor_at(b, d, v0, n):
-            m = keep.tile([P, n * P], F32, name=f"m{b}{d}{v0}", align_bytes=64)
+        def floor_at(b, d, v0, n, tag=""):
+            m = keep.tile([P, n * P], F32, name=f"m{b}{d}{v0}", tag=tag, align_bytes=64)
             tops[b, d, v0] = m
             nc.vector.scalar_tensor_tensor(
                 out=m[:], in0=accs["s", b][:, v0 * P : (v0 + n) * P], scalar=-1.0,
@@ -171,52 +175,80 @@ def tile_picked_wfilmg_relu_lo_kernel(
                     start=False, stop=(d == LISTS - 1 and i == n - 1), is_transpose=True,
                 )
 
-        def deal(b, v0, n):
-            nc.scalar.copy(
-                out=turned[:, v0 : v0 + n, :, b * Q : (b + 1) * Q],
-                in_=banks[b, v0][:, :n, :].rearrange("v i (q t) -> v i t q", t=PACK),
-            )
-
+        turned = [keep.tile([P, CHUNKS, P], F32, name=f"turned{b}") for b in range(BLOCKS)]
+        pairs = keep.tile([P, CHUNKS, 2, P, 2], BF16, name="pairs", align_bytes=64)
+        ys = [keep.tile([P, T], F32, name=f"y{b}") for b in range(BLOCKS)]
         y_codes = keep.tile([P, T], U32, name="y_codes", align_bytes=64)
         y_scales = keep.tile([P, T], U8, name="y_scales", align_bytes=64)
-        out_rows = out_0.rearrange("(p t) v -> p t v", t=PACK)
         out_words = out_1[0].rearrange("p c r -> p (c r)").bitcast(I32)
-        ys = {}
 
-        def turn_back(i):
-            bank = psum.tile([P, PACK, P], F32, name="back")
-            for t in range(PACK):
-                nc.tensor.transpose(bank[:, t, :], turned[:, i, t, :], ident[:])
-            y = keep.tile([P, PACK, P], F32, name=f"y{i}")
-            ys[i] = y
-            nc.scalar.copy(out=y[:], in_=bank[:])
-            nc.sync.dma_start(out=out_rows[:, :, i * P : (i + 1) * P], in_=y[:])
+        def leave_sum(b, v0, n):
+            nc.scalar.copy(out=turned[b][:, v0 : v0 + n, :], in_=banks[b, v0][:, :n, :])
 
-        def round_y(i):
-            nc.vector.tensor_copy(
-                out=rounded[:, i * P : (i + 1) * P, :].rearrange("p (c i) t -> p c t i", i=PACK),
-                in_=ys[i][:].rearrange("p t (c i) -> p c t i", i=PACK),
+        def round_pairs(src, b, v0, n):
+            nc.scalar.copy(
+                out=pairs[:, v0 : v0 + n, :, b * Q : (b + 1) * Q, :],
+                in_=src.rearrange("v i (q u e) -> v i u q e", u=2, e=2),
             )
 
-        def quantize_y(i, n):
-            cols = slice(i * P, (i + n) * P)
+        def turn_back(b, v0, n):
+            cols = slice(v0 * P, (v0 + n) * P)
+            bank = psum.tile([P, CHUNKS, P], F32, name="back")
+            for i in range(n):
+                nc.tensor.transpose(bank[:, i, :], turned[b][:, v0 + i, :], ident[:])
+            nc.scalar.copy(out=ys[b][:, cols], in_=bank[:, :n, :].rearrange("p i v -> p (i v)"))
+            nc.sync.dma_start(out=out_0[b * P : (b + 1) * P, cols], in_=ys[b][:, cols])
+
+        def planes(i):
+            cols = slice(i * P, (i + 1) * P)
+            bank = psum.tile([P, 2, P], F32, name="acc")
+            for u in range(2):
+                words = pairs[:, i, u, :, :].rearrange("v l e -> v (l e)").bitcast(F32)
+                nc.tensor.transpose(bank[:, u, :], words, ident[:])
+            grouped = keep.tile([P, P, PACK], BF16, name=f"y_grouped{i}", align_bytes=64)
+            nc.scalar.copy(
+                out=grouped[:].rearrange("p v (u e) -> p v u e", e=2).bitcast(F32).rearrange("p v u e -> p v (u e)"),
+                in_=bank[:].rearrange("p u v -> p v u"),
+            )
             nc.vector.quantize_mx(
                 out=y_codes[:, cols].bitcast(FP8X4), scales=y_scales[:, cols],
-                in_=rounded[:, cols, :].rearrange("p v t -> p (v t)"),
+                in_=grouped[:].rearrange("p v t -> p (v t)"),
             )
 
         cast(0)
         multiply(0)
         cast(1)
-        cast(2)
-        empty(0)
         multiply(1)
-        cast(3)
+        empty(0)
+        fetched = keep.tile([P, T], F32, name="fetched", tag="grp1", align_bytes=64)
+        nc.vector.tensor_copy(fetched[:], res["h", 0][:].indirect(lists[0][:]))
         empty(1)
+        cast(2)
         multiply(2)
-        cast(4)
+        cast(3)
+        gather(0, 1, 0, CHUNKS, "raw_s01")
+        multiply(3)
         empty(2)
-        for b in range(LAST):
+        cast(4)
+        gather(0, 2, 0, CHUNKS, "raw_h11")
+        first = keep.tile([P, T], F32, name="a000", align_bytes=64)
+        scaled[0, 0, 0] = first
+        nc.vector.tensor_tensor(first[:], fetched[:], res["g", 0][:], ALU.mult)
+        multiply(4)
+        empty(3)
+        cast(5)
+        empty(4)
+        cast(6)
+        open_sum(0, 0, CHUNKS)
+        for d in range(LISTS):
+            if d == 2:
+                multiply(5)
+                empty(5)
+                cast(7)
+            floor_at(0, d, 0, CHUNKS, "raw_g11" if d == 0 else "")
+            add_to_sum(0, d, 0, CHUNKS)
+        leave_sum(0, 0, CHUNKS)
+        for b in range(1, LAST):
             for d in range(LISTS):
                 i = LISTS * (b + 1) + d
                 kind, kb = products[i - 1]
@@ -226,12 +258,15 @@ def tile_picked_wfilmg_relu_lo_kernel(
                     floor_at(b, 0, 0, CHUNKS)
                     add_to_sum(b, 0, 0, CHUNKS)
                 multiply(i)
-                cast(i + 2)
                 empty(i)
+                cast(i + 2)
             for d in (1, 2):
                 floor_at(b, d, 0, CHUNKS)
                 add_to_sum(b, d, 0, CHUNKS)
-            deal(b, 0, CHUNKS)
+            leave_sum(b, 0, CHUNKS)
+        for b in range(LAST):
+            round_pairs(turned[b][:], b, 0, CHUNKS)
+            turn_back(b, 0, CHUNKS)
         for i in range(CHUNKS):
             for d in range(LISTS):
                 gather(LAST, d, i, 1, f"a{d}")
@@ -239,18 +274,13 @@ def tile_picked_wfilmg_relu_lo_kernel(
             for d in range(LISTS):
                 floor_at(LAST, d, i, 1)
                 add_to_sum(LAST, d, i, 1)
-            deal(LAST, i, 1)
-            turn_back(i)
-        rounded = keep.tile([P, T, PACK], BF16, name="rounded", tag="a2", align_bytes=64)
-        round_y(0)
-        round_y(1)
-        round_y(2)
-        quantize_y(0, 2)
-        nc.scalar.dma_start(out=out_words[:, : 2 * P], in_=y_codes[:, : 2 * P].bitcast(I32))
-        quantize_y(2, 1)
-        round_y(3)
-        quantize_y(3, 1)
-        nc.sync.dma_start(out=out_words[:, 2 * P :], in_=y_codes[:, 2 * P :].bitcast(I32))
+            round_pairs(banks[LAST, i][:, :1, :], LAST, i, 1)
+            leave_sum(LAST, i, 1)
+            planes(i)
+            turn_back(LAST, i, 1)
+            if i % 2 == 1:
+                both = slice((i - 1) * P, (i + 1) * P)
+                nc.sync.dma_start(out=out_words[:, both], in_=y_codes[:, both].bitcast(I32))
         for q in range(4):
             eng = nc.sync if q % 2 == 0 else nc.scalar
             eng.dma_start(

@@ -41,12 +41,8 @@ def tile_picked_wfilmg_relu_lo_kernel(
         xs = keep.tile([P, PASSES, T], U8, name="xs", align_bytes=64)
         xs_in = keep.tile([P, PASSES, T], U8, name="xs_in", align_bytes=64)
         ident = keep.tile([P, P], F32, name="ident")
-        warm = keep.tile([P, 8], F32, name="warm")
-        warm2 = keep.tile([P, 8], F32, name="warm2")
 
         nc.vector.memset(xs[:].rearrange("p z c -> p (z c)").bitcast(I32), 0)
-        nc.vector.memset(warm[:], 0.0)
-        nc.scalar.activation(out=warm2[:], in_=warm[:], func=COPY, scale=3.0)
         make_identity(nc, ident[:])
 
         weights = {"h": w3, "g": w1, "s": w2}
@@ -54,10 +50,16 @@ def tile_picked_wfilmg_relu_lo_kernel(
         raw = {}
 
         def load_w(kind, b):
+            if b > 0:
+                both = keep.tile([P, PASSES, PACK, P], F32, name=f"raw_{kind}{b}1", align_bytes=64)
+                raw[kind, b] = both
             for z in range(PASSES):
-                t = keep.tile([P, PACK, P], F32, name=f"raw_{kind}{b}{z}", align_bytes=64)
+                if b > 0:
+                    t = both[:, z, :, :]
+                else:
+                    t = keep.tile([P, PACK, P], F32, name=f"raw_{kind}{b}{z}", align_bytes=64)[:]
                 rows = weights[kind][z * P * PACK : (z + 1) * P * PACK, b * P : (b + 1) * P]
-                nc.sync.dma_start(out=t[:], in_=rows.rearrange("(p j) m -> p j m", j=PACK))
+                nc.sync.dma_start(out=t, in_=rows.rearrange("(p j) m -> p j m", j=PACK))
                 raw[kind, b, z] = t
 
         for q in range(4):
@@ -96,13 +98,19 @@ def tile_picked_wfilmg_relu_lo_kernel(
             kind, b = products[i]
             grouped = keep.tile([P, PASSES, P, PACK], BF16, name=f"grp{i}", tag="cod1" if i == 3 else f"grp{i}", align_bytes=64)
             grp[i] = grouped
+            if b > 0:
+                nc.scalar.copy(
+                    out=grouped[:].rearrange("p z (c i) j -> p z c j i", i=PACK),
+                    in_=raw[kind, b][:].rearrange("p z j (c i) -> p z c j i", i=PACK),
+                )
+                return
             for z in range(PASSES):
                 dst = grouped[:, z, :, :].rearrange("p (c i) j -> p c j i", i=PACK)
-                src = raw[kind, b, z][:].rearrange("p j (c i) -> p c j i", i=PACK)
+                src = raw[kind, b, z].rearrange("p j (c i) -> p c j i", i=PACK)
                 if (kind, b, z) in on_vector:
                     nc.vector.tensor_copy(out=dst, in_=src)
                 else:
-                    nc.scalar.copy(out=dst, in_=src)
+                    nc.scalar.activation(out=dst, in_=src, func=COPY)
 
         def multiply(i):
             kind, b = products[i]
@@ -267,20 +275,20 @@ def tile_picked_wfilmg_relu_lo_kernel(
         for b in range(LAST):
             round_pairs(turned[b][:], b, 0, CHUNKS)
             turn_back(b, 0, CHUNKS)
-        for i in range(CHUNKS):
+        for v0, n in ((0, 3), (3, 1)):
             for d in range(LISTS):
-                gather(LAST, d, i, 1, f"a{d}")
-            open_sum(LAST, i, 1)
+                gather(LAST, d, v0, n, f"a{d}")
+            open_sum(LAST, v0, n)
             for d in range(LISTS):
-                floor_at(LAST, d, i, 1)
-                add_to_sum(LAST, d, i, 1)
-            round_pairs(banks[LAST, i][:, :1, :], LAST, i, 1)
-            leave_sum(LAST, i, 1)
-            planes(i)
-            turn_back(LAST, i, 1)
-            if i % 2 == 1:
-                both = slice((i - 1) * P, (i + 1) * P)
-                nc.sync.dma_start(out=out_words[:, both], in_=y_codes[:, both].bitcast(I32))
+                floor_at(LAST, d, v0, n)
+                add_to_sum(LAST, d, v0, n)
+            round_pairs(banks[LAST, v0][:, :n, :], LAST, v0, n)
+            leave_sum(LAST, v0, n)
+            for i in range(v0, v0 + n):
+                planes(i)
+            turn_back(LAST, v0, n)
+            cols = slice(v0 * P, (v0 + n) * P)
+            nc.sync.dma_start(out=out_words[:, cols], in_=y_codes[:, cols].bitcast(I32))
         for q in range(4):
             eng = nc.sync if q % 2 == 0 else nc.scalar
             eng.dma_start(

@@ -50,11 +50,11 @@ def tile_picked_wfilmg_relu_lo_kernel(
         raw = {}
 
         def load_w(kind, b):
-            if b > 0:
+            if b > 1:
                 both = keep.tile([P, PASSES, PACK, P], F32, name=f"raw_{kind}{b}1", align_bytes=64)
                 raw[kind, b] = both
             for z in range(PASSES):
-                if b > 0:
+                if b > 1:
                     t = both[:, z, :, :]
                 else:
                     t = keep.tile([P, PACK, P], F32, name=f"raw_{kind}{b}{z}", align_bytes=64)[:]
@@ -86,7 +86,10 @@ def tile_picked_wfilmg_relu_lo_kernel(
         res = {}
         for b in range(BLOCKS):
             res["h", b] = keep.tile([P, T + SPARE], F32, name=f"h{b}")
-            nc.vector.memset(res["h", b][:, T:], 0.0)
+            if b == 0:
+                nc.vector.memset(res["h", b][:, T:], 0.0)
+            else:
+                nc.scalar.activation(out=res["h", b][:, T:], in_=res["h", 0][:, T:], func=COPY)
             res["g", b] = keep.tile([P, T], F32, name=f"g{b}")
             res["s", b] = keep.tile([P, T], F32, name=f"s{b}")
 
@@ -98,19 +101,19 @@ def tile_picked_wfilmg_relu_lo_kernel(
             kind, b = products[i]
             grouped = keep.tile([P, PASSES, P, PACK], BF16, name=f"grp{i}", tag="cod1" if i == 3 else f"grp{i}", align_bytes=64)
             grp[i] = grouped
-            if b > 0:
+            if b > 1:
                 nc.scalar.copy(
-                    out=grouped[:].rearrange("p z (c i) j -> p z c j i", i=PACK),
-                    in_=raw[kind, b][:].rearrange("p z j (c i) -> p z c j i", i=PACK),
+                    out=grouped[:].rearrange("p z (c i) j -> p z c j i", i=2),
+                    in_=raw[kind, b][:].rearrange("p z j (c i) -> p z c j i", i=2),
                 )
                 return
             for z in range(PASSES):
-                dst = grouped[:, z, :, :].rearrange("p (c i) j -> p c j i", i=PACK)
-                src = raw[kind, b, z].rearrange("p j (c i) -> p c j i", i=PACK)
+                dst = grouped[:, z, :, :].rearrange("p (c i) j -> p c j i", i=2)
+                src = raw[kind, b, z].rearrange("p j (c i) -> p c j i", i=2)
                 if (kind, b, z) in on_vector:
                     nc.vector.tensor_copy(out=dst, in_=src)
                 else:
-                    nc.scalar.activation(out=dst, in_=src, func=COPY)
+                    nc.scalar.copy(out=dst, in_=src)
 
         def multiply(i):
             kind, b = products[i]
@@ -275,7 +278,7 @@ def tile_picked_wfilmg_relu_lo_kernel(
         for b in range(LAST):
             round_pairs(turned[b][:], b, 0, CHUNKS)
             turn_back(b, 0, CHUNKS)
-        for v0, n in ((0, 3), (3, 1)):
+        for v0, n in ((0, 2), (2, 1), (3, 1)):
             for d in range(LISTS):
                 gather(LAST, d, v0, n, f"a{d}")
             open_sum(LAST, v0, n)
@@ -287,8 +290,9 @@ def tile_picked_wfilmg_relu_lo_kernel(
             for i in range(v0, v0 + n):
                 planes(i)
             turn_back(LAST, v0, n)
-            cols = slice(v0 * P, (v0 + n) * P)
-            nc.sync.dma_start(out=out_words[:, cols], in_=y_codes[:, cols].bitcast(I32))
+            if v0 != 2:
+                both = slice((v0 + n - 2) * P, (v0 + n) * P)
+                nc.sync.dma_start(out=out_words[:, both], in_=y_codes[:, both].bitcast(I32))
         for q in range(4):
             eng = nc.sync if q % 2 == 0 else nc.scalar
             eng.dma_start(

@@ -23,7 +23,9 @@ PASSES = K // (P * PACK)
 BLOCKS = N // P
 CHUNKS = T // P
 LISTS = 3
-SPARE = 192
+SPARE_FIRST = 192
+SPARE = 16
+SLOT = 2048
 Q = P // PACK
 LAST = BLOCKS - 1
 
@@ -34,6 +36,7 @@ def tile_picked_wfilmg_relu_lo_kernel(
     nc = tc.nc
     with ExitStack() as ctx:
         keep = ctx.enter_context(tc.tile_pool(name="keep", bufs=1))
+        tied = ctx.enter_context(tc.tile_pool(name="tied", bufs=1))
         psum = ctx.enter_context(tc.psum_pool(name="psum", bufs=2))
 
         lists = [keep.tile([P, T // 16], U16, name=f"list{d}") for d in range(LISTS)]
@@ -50,17 +53,18 @@ def tile_picked_wfilmg_relu_lo_kernel(
         raw = {}
 
         def load_w(kind, b):
-            if b > 1:
-                both = keep.tile([P, PASSES, PACK, P], F32, name=f"raw_{kind}{b}1", align_bytes=64)
-                raw[kind, b] = both
+            i = products.index((kind, b))
+            both = tied.tile([P, PASSES, PACK, P], F32, name=f"raw{i}", offset=2 * SLOT * i, align_bytes=64)
             for z in range(PASSES):
-                if b > 1:
-                    t = both[:, z, :, :]
-                else:
-                    t = keep.tile([P, PACK, P], F32, name=f"raw_{kind}{b}{z}", align_bytes=64)[:]
                 rows = weights[kind][z * P * PACK : (z + 1) * P * PACK, b * P : (b + 1) * P]
-                nc.sync.dma_start(out=t, in_=rows.rearrange("(p j) m -> p j m", j=PACK))
-                raw[kind, b, z] = t
+                nc.sync.dma_start(out=both[:, z, :, :], in_=rows.rearrange("(p j) m -> p j m", j=PACK))
+                raw[kind, b, z] = both[:, z, :, :]
+
+        def after_cast(name, i, half):
+            return tied.tile([P, T], F32, name=name, offset=(2 * i + half) * SLOT, align_bytes=64)
+
+        def after_quantise(name, i):
+            return keep.tile([P, T], F32, name=name, tag=f"grp{i}", align_bytes=64)
 
         for q in range(4):
             nc.sync.dma_start(
@@ -85,11 +89,11 @@ def tile_picked_wfilmg_relu_lo_kernel(
 
         res = {}
         for b in range(BLOCKS):
-            res["h", b] = keep.tile([P, T + SPARE], F32, name=f"h{b}")
+            res["h", b] = keep.tile([P, T + (SPARE if b else SPARE_FIRST)], F32, name=f"h{b}")
             if b == 0:
                 nc.vector.memset(res["h", b][:, T:], 0.0)
             else:
-                nc.scalar.activation(out=res["h", b][:, T:], in_=res["h", 0][:, T:], func=COPY)
+                nc.scalar.activation(out=res["h", b][:, T:], in_=res["h", 0][:, T : T + SPARE], func=COPY)
             res["g", b] = keep.tile([P, T], F32, name=f"g{b}")
             res["s", b] = keep.tile([P, T], F32, name=f"s{b}")
 
@@ -101,12 +105,6 @@ def tile_picked_wfilmg_relu_lo_kernel(
             kind, b = products[i]
             grouped = keep.tile([P, PASSES, P, PACK], BF16, name=f"grp{i}", tag="cod1" if i == 3 else f"grp{i}", align_bytes=64)
             grp[i] = grouped
-            if b > 1:
-                nc.scalar.copy(
-                    out=grouped[:].rearrange("p z (c i) j -> p z c j i", i=2),
-                    in_=raw[kind, b][:].rearrange("p z j (c i) -> p z c j i", i=2),
-                )
-                return
             for z in range(PASSES):
                 dst = grouped[:, z, :, :].rearrange("p (c i) j -> p c j i", i=2)
                 src = raw[kind, b, z].rearrange("p j (c i) -> p c j i", i=2)
@@ -152,8 +150,7 @@ def tile_picked_wfilmg_relu_lo_kernel(
             else:
                 nc.scalar.copy(out=res[kind, b][:, :T], in_=accs[kind, b][:])
 
-        def gather(b, d, v0, n, tag):
-            a = keep.tile([P, T], F32, name=f"a{b}{d}{v0}", tag=tag, align_bytes=64)
+        def gather(b, d, v0, n, a):
             scaled[b, d, v0] = a
             nc.vector.tensor_tensor(
                 a[:, : n * P],
@@ -162,11 +159,10 @@ def tile_picked_wfilmg_relu_lo_kernel(
                 ALU.mult,
             )
 
-        def floor_at(b, d, v0, n, tag=""):
-            m = keep.tile([P, n * P], F32, name=f"m{b}{d}{v0}", tag=tag, align_bytes=64)
+        def floor_at(b, d, v0, n, m):
             tops[b, d, v0] = m
             nc.vector.scalar_tensor_tensor(
-                out=m[:], in0=accs["s", b][:, v0 * P : (v0 + n) * P], scalar=-1.0,
+                out=m[:, : n * P], in0=accs["s", b][:, v0 * P : (v0 + n) * P], scalar=-1.0,
                 in1=scaled[b, d, v0][:, : n * P], op0=ALU.mult, op1=ALU.max,
             )
 
@@ -179,11 +175,11 @@ def tile_picked_wfilmg_relu_lo_kernel(
                     start=(i == 0), stop=False, is_transpose=True,
                 )
 
-        def add_to_sum(b, d, v0, n):
+        def add_to_sum(b, d, v0, n, last):
             for i in range(n):
                 nc.tensor.matmul(
                     banks[b, v0][:, i, :], lhsT=tops[b, d, v0][:, i * P : (i + 1) * P], rhs=ident[:],
-                    start=False, stop=(d == LISTS - 1 and i == n - 1), is_transpose=True,
+                    start=False, stop=(last and i == n - 1), is_transpose=True,
                 )
 
         turned = [keep.tile([P, CHUNKS, P], F32, name=f"turned{b}") for b in range(BLOCKS)]
@@ -237,54 +233,60 @@ def tile_picked_wfilmg_relu_lo_kernel(
         cast(2)
         multiply(2)
         cast(3)
-        gather(0, 1, 0, CHUNKS, "raw_s01")
+        gather(0, 1, 0, CHUNKS, after_cast("a01", 2, 0))
         multiply(3)
         empty(2)
         cast(4)
-        gather(0, 2, 0, CHUNKS, "raw_h11")
-        first = keep.tile([P, T], F32, name="a000", align_bytes=64)
-        scaled[0, 0, 0] = first
-        nc.vector.tensor_tensor(first[:], fetched[:], res["g", 0][:], ALU.mult)
+        gather(0, 2, 0, CHUNKS, after_cast("a02", 3, 0))
         multiply(4)
         empty(3)
         cast(5)
         empty(4)
         cast(6)
+        scaled[0, 0, 0] = after_cast("a00", 4, 0)
+        nc.vector.tensor_tensor(scaled[0, 0, 0][:], fetched[:], res["g", 0][:], ALU.mult)
         open_sum(0, 0, CHUNKS)
-        for d in range(LISTS):
-            if d == 2:
-                multiply(5)
-                empty(5)
-                cast(7)
-            floor_at(0, d, 0, CHUNKS, "raw_g11" if d == 0 else "")
-            add_to_sum(0, d, 0, CHUNKS)
-        leave_sum(0, 0, CHUNKS)
+        floor_at(0, 1, 0, CHUNKS, after_cast("m01", 4, 1))
+        add_to_sum(0, 1, 0, CHUNKS, False)
+        floor_at(0, 2, 0, CHUNKS, after_quantise("m02", 4))
+        add_to_sum(0, 2, 0, CHUNKS, False)
+        multiply(5)
+        empty(5)
+        cast(7)
+        waiting = (0, 0)
         for b in range(1, LAST):
             for d in range(LISTS):
                 i = LISTS * (b + 1) + d
-                kind, kb = products[i - 1]
-                gather(b, d, 0, CHUNKS, f"raw_{kind}{kb}1")
-                if d == 2:
-                    open_sum(b, 0, CHUNKS)
-                    floor_at(b, 0, 0, CHUNKS)
-                    add_to_sum(b, 0, 0, CHUNKS)
+                gather(b, d, 0, CHUNKS, after_cast(f"a{b}{d}", i - 1, 0))
                 multiply(i)
                 empty(i)
                 cast(i + 2)
-            for d in (1, 2):
-                floor_at(b, d, 0, CHUNKS)
-                add_to_sum(b, d, 0, CHUNKS)
-            leave_sum(b, 0, CHUNKS)
-        for b in range(LAST):
-            round_pairs(turned[b][:], b, 0, CHUNKS)
-            turn_back(b, 0, CHUNKS)
+                if d == 1:
+                    open_sum(b, 0, CHUNKS)
+                floor_at(*waiting, 0, CHUNKS, after_cast(f"m{waiting[0]}{waiting[1]}", i, 1))
+                add_to_sum(*waiting, 0, CHUNKS, d == 0)
+                if d == 0:
+                    leave_sum(b - 1, 0, CHUNKS)
+                waiting = (b, d)
+        final = len(products) - 1
         for v0, n in ((0, 2), (2, 1), (3, 1)):
             for d in range(LISTS):
-                gather(LAST, d, v0, n, f"a{d}")
+                if d == 0:
+                    a = after_cast(f"a{LAST}0{v0}", final, 0)
+                else:
+                    a = keep.tile([P, T], F32, name=f"a{LAST}{d}{v0}", tag=f"a{d}", align_bytes=64)
+                gather(LAST, d, v0, n, a)
+                if v0 == 0 and d == 0:
+                    floor_at(*waiting, 0, CHUNKS, after_quantise("m_last", final))
+                    add_to_sum(*waiting, 0, CHUNKS, True)
+                    leave_sum(LAST - 1, 0, CHUNKS)
+                    for b in range(LAST):
+                        round_pairs(turned[b][:], b, 0, CHUNKS)
+                        turn_back(b, 0, CHUNKS)
             open_sum(LAST, v0, n)
             for d in range(LISTS):
-                floor_at(LAST, d, v0, n)
-                add_to_sum(LAST, d, v0, n)
+                floor_at(LAST, d, v0, n, keep.tile([P, n * P], F32, name=f"m{LAST}{d}{v0}", align_bytes=64))
+                add_to_sum(LAST, d, v0, n, d == LISTS - 1)
             round_pairs(banks[LAST, v0][:, :n, :], LAST, v0, n)
             leave_sum(LAST, v0, n)
             for i in range(v0, v0 + n):

@@ -25,7 +25,8 @@ CHUNKS = T // P
 LISTS = 3
 SPARE_FIRST = 192
 SPARE = 16
-SLOT = 2048
+SLOT = 2176
+PLACES = 4
 Q = P // PACK
 LAST = BLOCKS - 1
 
@@ -50,21 +51,20 @@ def tile_picked_wfilmg_relu_lo_kernel(
 
         weights = {"h": w3, "g": w1, "s": w2}
         products = [(kind, b) for b in range(BLOCKS) for kind in "hgs"]
+        final = len(products) - 1
         raw = {}
 
         def load_w(kind, b):
             i = products.index((kind, b))
-            both = tied.tile([P, PASSES, PACK, P], F32, name=f"raw{i}", offset=2 * SLOT * i, align_bytes=64)
+            room = tied.tile([P, PLACES * SLOT // 4], F32, name=f"raw{i}", offset=PLACES * i * SLOT, align_bytes=64)
+            both = room[:, : PASSES * PACK * P].rearrange("p (z j m) -> p z j m", z=PASSES, j=PACK)
             for z in range(PASSES):
                 rows = weights[kind][z * P * PACK : (z + 1) * P * PACK, b * P : (b + 1) * P]
                 nc.sync.dma_start(out=both[:, z, :, :], in_=rows.rearrange("(p j) m -> p j m", j=PACK))
                 raw[kind, b, z] = both[:, z, :, :]
 
-        def after_cast(name, i, half):
-            return tied.tile([P, T], F32, name=name, offset=(2 * i + half) * SLOT, align_bytes=64)
-
-        def after_quantise(name, i):
-            return keep.tile([P, T], F32, name=name, tag=f"grp{i}", align_bytes=64)
+        def after_cast(name, i, place, width=T):
+            return tied.tile([P, width], F32, name=name, offset=(PLACES * i + place) * SLOT, align_bytes=64)
 
         for q in range(4):
             nc.sync.dma_start(
@@ -86,16 +86,15 @@ def tile_picked_wfilmg_relu_lo_kernel(
                 out=xs[32 * q : 32 * q + 4, :, :].bitcast(I32), in_=xs_in[32 * q : 32 * q + 4, :, :].bitcast(I32)
             )
         on_vector = [("h", 0, 1), ("g", 0, 1)]
+        on_gpsimd = [5, 8]
+        grp_tag = {3: "cod1", 5: "g0", 6: "cod4", 8: "g1", 9: "cod7"}
 
-        res = {}
+        zeros = keep.tile([P, SPARE_FIRST], F32, name="zeros")
+        nc.vector.memset(zeros[:], 0.0)
+        res = {("h", 0): keep.tile([P, T + SPARE_FIRST], F32, name="h0")}
+        nc.scalar.activation(out=res["h", 0][:, T:], in_=zeros[:], func=COPY)
         for b in range(BLOCKS):
-            res["h", b] = keep.tile([P, T + (SPARE if b else SPARE_FIRST)], F32, name=f"h{b}")
-            if b == 0:
-                nc.vector.memset(res["h", b][:, T:], 0.0)
-            else:
-                nc.scalar.activation(out=res["h", b][:, T:], in_=res["h", 0][:, T : T + SPARE], func=COPY)
-            res["g", b] = keep.tile([P, T], F32, name=f"g{b}")
-            res["s", b] = keep.tile([P, T], F32, name=f"s{b}")
+            res["g", b] = keep.tile([P, T], F32, name=f"g{b}", tag=f"g{b}", align_bytes=64)
 
         grp, accs, banks, tops, scaled = {}, {}, {}, {}, {}
 
@@ -103,9 +102,14 @@ def tile_picked_wfilmg_relu_lo_kernel(
             if i >= len(products):
                 return
             kind, b = products[i]
-            grouped = keep.tile([P, PASSES, P, PACK], BF16, name=f"grp{i}", tag="cod1" if i == 3 else f"grp{i}", align_bytes=64)
+            grouped = keep.tile([P, PASSES, P, PACK], BF16, name=f"grp{i}", tag=grp_tag.get(i, f"grp{i}"), align_bytes=64)
             grp[i] = grouped
             for z in range(PASSES):
+                if i in on_gpsimd:
+                    nc.gpsimd.tensor_scalar(
+                        grouped[:, z, :, :], raw[kind, b, z].rearrange("p j m -> p m j"), 1.0, 0.0, ALU.mult, ALU.add
+                    )
+                    continue
                 dst = grouped[:, z, :, :].rearrange("p (c i) j -> p c j i", i=2)
                 src = raw[kind, b, z].rearrange("p j (c i) -> p c j i", i=2)
                 if (kind, b, z) in on_vector:
@@ -145,7 +149,11 @@ def tile_picked_wfilmg_relu_lo_kernel(
 
         def empty(i):
             kind, b = products[i]
+            if kind == "h" and b > 0:
+                res[kind, b] = after_cast(f"h{b}", *((i + 1, 2) if b < LAST else (final, 3)), T + SPARE)
+                nc.gpsimd.memset(res[kind, b][:, T:], 0.0)
             if kind == "s":
+                res[kind, b] = keep.tile([P, T], F32, name=f"s{b}")
                 nc.scalar.activation(out=res["s", b][:], in_=accs[kind, b][:], func=COPY, scale=float(LISTS))
             else:
                 nc.scalar.copy(out=res[kind, b][:, :T], in_=accs[kind, b][:])
@@ -166,24 +174,21 @@ def tile_picked_wfilmg_relu_lo_kernel(
                 in1=scaled[b, d, v0][:, : n * P], op0=ALU.mult, op1=ALU.max,
             )
 
-        def open_sum(b, v0, n):
-            bank = psum.tile([P, CHUNKS, P], F32, name="sum")
-            banks[b, v0] = bank
+        def add_to_sum(b, term, v0, n, first, last):
+            if first:
+                banks[b, v0] = psum.tile([P, CHUNKS, P], F32, name="sum")
             for i in range(n):
                 nc.tensor.matmul(
-                    bank[:, i, :], lhsT=res["s", b][:, (v0 + i) * P : (v0 + i + 1) * P], rhs=ident[:],
-                    start=(i == 0), stop=False, is_transpose=True,
+                    banks[b, v0][:, i, :], lhsT=term[:, i * P : (i + 1) * P], rhs=ident[:],
+                    start=(first and i == 0), stop=(last and i == n - 1), is_transpose=True,
                 )
 
-        def add_to_sum(b, d, v0, n, last):
-            for i in range(n):
-                nc.tensor.matmul(
-                    banks[b, v0][:, i, :], lhsT=tops[b, d, v0][:, i * P : (i + 1) * P], rhs=ident[:],
-                    start=False, stop=(last and i == n - 1), is_transpose=True,
-                )
+        def close_sum(b):
+            empty(LISTS * b + 2)
+            add_to_sum(b, res["s", b], 0, CHUNKS, False, True)
+            leave_sum(b, 0, CHUNKS)
 
         turned = [keep.tile([P, CHUNKS, P], F32, name=f"turned{b}") for b in range(BLOCKS)]
-        pairs = keep.tile([P, CHUNKS, 2, P, 2], BF16, name="pairs", align_bytes=64)
         ys = [keep.tile([P, T], F32, name=f"y{b}") for b in range(BLOCKS)]
         y_codes = keep.tile([P, T], U32, name="y_codes", align_bytes=64)
         y_scales = keep.tile([P, T], U8, name="y_scales", align_bytes=64)
@@ -193,6 +198,13 @@ def tile_picked_wfilmg_relu_lo_kernel(
             nc.scalar.copy(out=turned[b][:, v0 : v0 + n, :], in_=banks[b, v0][:, :n, :])
 
         def round_pairs(src, b, v0, n):
+            if b < 2:
+                nc.gpsimd.tensor_scalar(
+                    pairs[:, v0 : v0 + n, :, b * Q : (b + 1) * Q, :].rearrange("v i u q e -> v u i q e"),
+                    src.rearrange("v i (q u e) -> v u i q e", u=2, e=2),
+                    1.0, 0.0, ALU.mult, ALU.add,
+                )
+                return
             nc.scalar.copy(
                 out=pairs[:, v0 : v0 + n, :, b * Q : (b + 1) * Q, :],
                 in_=src.rearrange("v i (q u e) -> v i u q e", u=2, e=2),
@@ -231,62 +243,65 @@ def tile_picked_wfilmg_relu_lo_kernel(
         nc.vector.tensor_copy(fetched[:], res["h", 0][:].indirect(lists[0][:]))
         empty(1)
         cast(2)
+        gather(0, 1, 0, CHUNKS, keep.tile([P, T], F32, name="a01", align_bytes=64))
         multiply(2)
         cast(3)
-        gather(0, 1, 0, CHUNKS, after_cast("a01", 2, 0))
-        multiply(3)
-        empty(2)
         cast(4)
-        gather(0, 2, 0, CHUNKS, after_cast("a02", 3, 0))
+        gather(0, 2, 0, CHUNKS, after_cast("a02", 2, 0))
+        multiply(3)
         multiply(4)
         empty(3)
-        cast(5)
         empty(4)
-        cast(6)
         scaled[0, 0, 0] = after_cast("a00", 4, 0)
         nc.vector.tensor_tensor(scaled[0, 0, 0][:], fetched[:], res["g", 0][:], ALU.mult)
-        open_sum(0, 0, CHUNKS)
+        cast(5)
+        cast(6)
         floor_at(0, 1, 0, CHUNKS, after_cast("m01", 4, 1))
-        add_to_sum(0, 1, 0, CHUNKS, False)
-        floor_at(0, 2, 0, CHUNKS, after_quantise("m02", 4))
-        add_to_sum(0, 2, 0, CHUNKS, False)
-        multiply(5)
-        empty(5)
+        add_to_sum(0, tops[0, 1, 0], 0, CHUNKS, True, False)
+        floor_at(0, 2, 0, CHUNKS, after_cast("m02", 4, 3))
+        add_to_sum(0, tops[0, 2, 0], 0, CHUNKS, False, False)
+        floor_at(0, 0, 0, CHUNKS, keep.tile([P, T], F32, name="m00", align_bytes=64))
+        add_to_sum(0, tops[0, 0, 0], 0, CHUNKS, False, False)
         cast(7)
-        waiting = (0, 0)
+        close_sum(0)
         for b in range(1, LAST):
+            shift, h_next, g_next = LISTS * b + 2, LISTS * b + 3, LISTS * b + 4
+            gather(b, 0, 0, CHUNKS, keep.tile([P, T], F32, name=f"a{b}0", align_bytes=64))
+            multiply(shift)
+            multiply(h_next)
+            wide = tied.tile([P, SLOT // 2], F32, name=f"a{b}1", offset=(PLACES * h_next - 1) * SLOT, align_bytes=64)
+            gather(b, 1, 0, CHUNKS, wide)
+            multiply(g_next)
+            if b == LAST - 1:
+                cast(final)
+            empty(h_next)
+            empty(g_next)
+            gather(b, 2, 0, CHUNKS, after_cast(f"a{b}2", g_next, 0))
+            if b == LAST - 1:
+                multiply(g_next + 1)
+                empty(g_next + 1)
+                tiles = [after_cast(f"m{b}{d}", g_next + 1, d) for d in range(LISTS)]
+            else:
+                cast(g_next + 1)
+                cast(g_next + 2)
+                cast(g_next + 3)
+                tiles = [after_cast(f"m{b}0", g_next, 1), after_cast(f"m{b}1", g_next, 3)]
+                tiles.append(keep.tile([P, T], F32, name=f"m{b}2", align_bytes=64))
             for d in range(LISTS):
-                i = LISTS * (b + 1) + d
-                gather(b, d, 0, CHUNKS, after_cast(f"a{b}{d}", i - 1, 0))
-                multiply(i)
-                empty(i)
-                cast(i + 2)
-                if d == 1:
-                    open_sum(b, 0, CHUNKS)
-                floor_at(*waiting, 0, CHUNKS, after_cast(f"m{waiting[0]}{waiting[1]}", i, 1))
-                add_to_sum(*waiting, 0, CHUNKS, d == 0)
-                if d == 0:
-                    leave_sum(b - 1, 0, CHUNKS)
-                waiting = (b, d)
-        final = len(products) - 1
+                floor_at(b, d, 0, CHUNKS, tiles[d])
+                add_to_sum(b, tops[b, d, 0], 0, CHUNKS, d == 0, False)
+            close_sum(b)
+        pairs = keep.tile([P, CHUNKS, 2, P, 2], BF16, name="pairs", tag="grp11", align_bytes=64)
+        for b in range(LAST):
+            round_pairs(turned[b][:], b, 0, CHUNKS)
+            turn_back(b, 0, CHUNKS)
         for v0, n in ((0, 2), (2, 1), (3, 1)):
             for d in range(LISTS):
-                if d == 0:
-                    a = after_cast(f"a{LAST}0{v0}", final, 0)
-                else:
-                    a = keep.tile([P, T], F32, name=f"a{LAST}{d}{v0}", tag=f"a{d}", align_bytes=64)
-                gather(LAST, d, v0, n, a)
-                if v0 == 0 and d == 0:
-                    floor_at(*waiting, 0, CHUNKS, after_quantise("m_last", final))
-                    add_to_sum(*waiting, 0, CHUNKS, True)
-                    leave_sum(LAST - 1, 0, CHUNKS)
-                    for b in range(LAST):
-                        round_pairs(turned[b][:], b, 0, CHUNKS)
-                        turn_back(b, 0, CHUNKS)
-            open_sum(LAST, v0, n)
+                gather(LAST, d, v0, n, keep.tile([P, T], F32, name=f"a{LAST}{d}{v0}", tag=f"a{d}", align_bytes=64))
+            add_to_sum(LAST, res["s", LAST][:, v0 * P :], v0, n, True, False)
             for d in range(LISTS):
                 floor_at(LAST, d, v0, n, keep.tile([P, n * P], F32, name=f"m{LAST}{d}{v0}", align_bytes=64))
-                add_to_sum(LAST, d, v0, n, d == LISTS - 1)
+                add_to_sum(LAST, tops[LAST, d, v0], v0, n, False, d == LISTS - 1)
             round_pairs(banks[LAST, v0][:, :n, :], LAST, v0, n)
             leave_sum(LAST, v0, n)
             for i in range(v0, v0 + n):

@@ -105,7 +105,7 @@ def tile_picked_wfilmg_relu_lo_kernel(
             grouped = keep.tile([P, PASSES, P, PACK], BF16, name=f"grp{i}", tag=grp_tag.get(i, f"grp{i}"), align_bytes=64)
             grp[i] = grouped
             for z in range(PASSES):
-                if i in on_gpsimd:
+                if i in on_gpsimd and z == 0:
                     nc.gpsimd.tensor_scalar(
                         grouped[:, z, :, :], raw[kind, b, z].rearrange("p j m -> p m j"), 1.0, 0.0, ALU.mult, ALU.add
                     )
@@ -198,7 +198,7 @@ def tile_picked_wfilmg_relu_lo_kernel(
             nc.scalar.copy(out=turned[b][:, v0 : v0 + n, :], in_=banks[b, v0][:, :n, :])
 
         def round_pairs(src, b, v0, n):
-            if b < 2:
+            if b == 0:
                 nc.gpsimd.tensor_scalar(
                     pairs[:, v0 : v0 + n, :, b * Q : (b + 1) * Q, :].rearrange("v i u q e -> v u i q e"),
                     src.rearrange("v i (q u e) -> v u i q e", u=2, e=2),
@@ -215,7 +215,10 @@ def tile_picked_wfilmg_relu_lo_kernel(
             bank = psum.tile([P, CHUNKS, P], F32, name="back")
             for i in range(n):
                 nc.tensor.transpose(bank[:, i, :], turned[b][:, v0 + i, :], ident[:])
-            nc.scalar.copy(out=ys[b][:, cols], in_=bank[:, :n, :].rearrange("p i v -> p (i v)"))
+            if v0 > 0:
+                nc.vector.tensor_copy(out=ys[b][:, cols], in_=bank[:, :n, :].rearrange("p i v -> p (i v)"))
+            else:
+                nc.scalar.copy(out=ys[b][:, cols], in_=bank[:, :n, :].rearrange("p i v -> p (i v)"))
             nc.sync.dma_start(out=out_0[b * P : (b + 1) * P, cols], in_=ys[b][:, cols])
 
         def planes(i):

@@ -23,12 +23,11 @@ PASSES = K // (P * PACK)
 BLOCKS = N // P
 CHUNKS = T // P
 LISTS = 3
-SPARE_FIRST = 192
 SPARE = 16
-SLOT = 2176
-PLACES = 4
 Q = P // PACK
 LAST = BLOCKS - 1
+KIB = 1024
+PIECES = ((0, 2), (2, 1), (3, 1))
 
 
 def tile_picked_wfilmg_relu_lo_kernel(
@@ -50,21 +49,14 @@ def tile_picked_wfilmg_relu_lo_kernel(
         make_identity(nc, ident[:])
 
         weights = {"h": w3, "g": w1, "s": w2}
-        products = [(kind, b) for b in range(BLOCKS) for kind in "hgs"]
-        final = len(products) - 1
         raw = {}
 
         def load_w(kind, b):
-            i = products.index((kind, b))
-            room = tied.tile([P, PLACES * SLOT // 4], F32, name=f"raw{i}", offset=PLACES * i * SLOT, align_bytes=64)
-            both = room[:, : PASSES * PACK * P].rearrange("p (z j m) -> p z j m", z=PASSES, j=PACK)
+            both = keep.tile([P, PASSES, PACK, P], F32, name=f"raw_{kind}{b}", align_bytes=64)
+            raw[kind, b] = both
             for z in range(PASSES):
                 rows = weights[kind][z * P * PACK : (z + 1) * P * PACK, b * P : (b + 1) * P]
                 nc.sync.dma_start(out=both[:, z, :, :], in_=rows.rearrange("(p j) m -> p j m", j=PACK))
-                raw[kind, b, z] = both[:, z, :, :]
-
-        def after_cast(name, i, place, width=T):
-            return tied.tile([P, width], F32, name=name, offset=(PLACES * i + place) * SLOT, align_bytes=64)
 
         for q in range(4):
             nc.sync.dma_start(
@@ -76,63 +68,64 @@ def tile_picked_wfilmg_relu_lo_kernel(
         load_w("g", 0)
         nc.sync.dma_start(lists[0][:], pos1)
         load_w("s", 0)
-        nc.sync.dma_start(lists[1][:], pos2)
         load_w("h", 1)
+        nc.sync.dma_start(lists[1][:], pos2)
         nc.sync.dma_start(lists[2][:], pos3)
-        for kind, b in products[4:]:
-            load_w(kind, b)
+        for b in range(1, BLOCKS):
+            load_w("g", b)
+            load_w("s", b)
+            if b < LAST:
+                load_w("h", b + 1)
         for q in range(4):
             nc.vector.tensor_copy(
                 out=xs[32 * q : 32 * q + 4, :, :].bitcast(I32), in_=xs_in[32 * q : 32 * q + 4, :, :].bitcast(I32)
             )
-        on_vector = [("h", 0, 1), ("g", 0, 1)]
-        on_gpsimd = [5, 8]
-        grp_tag = {3: "cod1", 5: "g0", 6: "cod4", 8: "g1", 9: "cod7"}
 
-        zeros = keep.tile([P, SPARE_FIRST], F32, name="zeros")
+        hs = [keep.tile([P, T + SPARE], F32, name=f"h{b}") for b in range(BLOCKS)]
+        zeros = keep.tile([P, SPARE], F32, name="zeros")
         nc.vector.memset(zeros[:], 0.0)
-        res = {("h", 0): keep.tile([P, T + SPARE_FIRST], F32, name="h0")}
-        nc.scalar.activation(out=res["h", 0][:, T:], in_=zeros[:], func=COPY)
-        for b in range(BLOCKS):
-            res["g", b] = keep.tile([P, T], F32, name=f"g{b}", tag=f"g{b}", align_bytes=64)
+        nc.scalar.activation(out=hs[0][:, T:], in_=zeros[:], func=COPY)
+        for b in range(1, BLOCKS):
+            nc.gpsimd.memset(hs[b][:, T:], 0.0)
 
-        grp, accs, banks, tops, scaled = {}, {}, {}, {}, {}
+        grp, accs, banks = {}, {}, {}
 
-        def cast(i):
-            if i >= len(products):
-                return
-            kind, b = products[i]
-            grouped = keep.tile([P, PASSES, P, PACK], BF16, name=f"grp{i}", tag=grp_tag.get(i, f"grp{i}"), align_bytes=64)
-            grp[i] = grouped
-            for z in range(PASSES):
-                if i in on_gpsimd and z == 0:
-                    nc.gpsimd.tensor_scalar(
-                        grouped[:, z, :, :], raw[kind, b, z].rearrange("p j m -> p m j"), 1.0, 0.0, ALU.mult, ALU.add
-                    )
-                    continue
+        def placed(offset, shape, dtype, name):
+            return tied.tile(shape, dtype, name=name, offset=offset, align_bytes=64)
+
+        def own(shape, dtype, name, tag=None):
+            return keep.tile(shape, dtype, name=name, tag=tag or name, align_bytes=64)
+
+        def cast(kind, b, engines, grouped):
+            grp[kind, b] = grouped
+            for z, eng in enumerate(engines):
                 dst = grouped[:, z, :, :].rearrange("p (c i) j -> p c j i", i=2)
-                src = raw[kind, b, z].rearrange("p j (c i) -> p c j i", i=2)
-                if (kind, b, z) in on_vector:
+                src = raw[kind, b][:, z, :, :].rearrange("p j (c i) -> p c j i", i=2)
+                if eng == "v":
                     nc.vector.tensor_copy(out=dst, in_=src)
                 else:
                     nc.scalar.copy(out=dst, in_=src)
 
-        def multiply(i):
-            kind, b = products[i]
-            codes = keep.tile([P, PASSES, P], U32, name=f"cod{i}", tag=f"cod{i}", align_bytes=64)
+        def cast_on_gpsimd(kind, b, grouped):
+            grp[kind, b] = grouped
+            nc.gpsimd.tensor_scalar(
+                grouped, raw[kind, b][:].rearrange("p z j m -> p z m j"), 1.0, 0.0, ALU.mult, ALU.add
+            )
+
+        def multiply(kind, b, codes, by_pass=False):
             scales = keep.tile([P, PASSES, P], U8, name=f"scl_{kind}{b}", align_bytes=64)
-            if i < 2:
+            if by_pass:
                 for z in range(PASSES):
                     nc.vector.quantize_mx(
                         out=codes[:, z, :].bitcast(FP8X4),
                         scales=scales[:, z, :],
-                        in_=grp[i][:, z, :, :].rearrange("p m j -> p (m j)"),
+                        in_=grp[kind, b][:, z, :, :].rearrange("p m j -> p (m j)"),
                     )
             else:
                 nc.vector.quantize_mx(
                     out=codes[:].rearrange("p z m -> p (z m)").bitcast(FP8X4),
                     scales=scales[:].rearrange("p z m -> p (z m)"),
-                    in_=grp[i][:].rearrange("p z m j -> p (z m j)"),
+                    in_=grp[kind, b].rearrange("p z m j -> p (z m j)"),
                 )
             acc = psum.tile([P, T], F32, name="shift" if kind == "s" else "acc")
             accs[kind, b] = acc
@@ -147,83 +140,73 @@ def tile_picked_wfilmg_relu_lo_kernel(
                     stop=(z == PASSES - 1),
                 )
 
-        def empty(i):
-            kind, b = products[i]
-            if kind == "h" and b > 0:
-                res[kind, b] = after_cast(f"h{b}", *((i + 1, 2) if b < LAST else (final, 3)), T + SPARE)
-                nc.gpsimd.memset(res[kind, b][:, T:], 0.0)
-            if kind == "s":
-                res[kind, b] = keep.tile([P, T], F32, name=f"s{b}")
-                nc.scalar.activation(out=res["s", b][:], in_=accs[kind, b][:], func=COPY, scale=float(LISTS))
-            else:
-                nc.scalar.copy(out=res[kind, b][:, :T], in_=accs[kind, b][:])
+        fetched = {}
 
-        def gather(b, d, v0, n, a):
-            scaled[b, d, v0] = a
-            nc.vector.tensor_tensor(
-                a[:, : n * P],
-                res["h", b][:].indirect(lists[d][:, v0 * 8 : (v0 + n) * 8]),
-                res["g", b][:, v0 * P : (v0 + n) * P],
-                ALU.mult,
-            )
-
-        def floor_at(b, d, v0, n, m):
-            tops[b, d, v0] = m
-            nc.vector.scalar_tensor_tensor(
-                out=m[:, : n * P], in0=accs["s", b][:, v0 * P : (v0 + n) * P], scalar=-1.0,
-                in1=scaled[b, d, v0][:, : n * P], op0=ALU.mult, op1=ALU.max,
-            )
+        def fetch(b, pieces):
+            nc.scalar.copy(out=hs[b][:, :T], in_=accs["h", b][:])
+            for v0, n in pieces:
+                if n == CHUNKS:
+                    rows = [own([P, T], F32, f"fetched{b}{d}", f"fetched{b}{d}")[:] for d in range(LISTS)]
+                    fetched[b] = rows
+                else:
+                    fetched[b, v0] = own([P, LISTS, n * P], F32, f"fetched{b}{v0}")
+                    rows = [fetched[b, v0][:, d, :] for d in range(LISTS)]
+                for d in range(LISTS):
+                    nc.scalar.activation(
+                        out=rows[d], in_=hs[b][:].indirect(lists[d][:, v0 * 8 : (v0 + n) * 8]), func=COPY
+                    )
 
         def add_to_sum(b, term, v0, n, first, last):
             if first:
-                banks[b, v0] = psum.tile([P, CHUNKS, P], F32, name="sum")
+                banks[b, v0] = psum.tile([P, CHUNKS, P], F32, name={0: "sum", 2: "acc", 3: "shift"}[v0])
             for i in range(n):
                 nc.tensor.matmul(
                     banks[b, v0][:, i, :], lhsT=term[:, i * P : (i + 1) * P], rhs=ident[:],
                     start=(first and i == 0), stop=(last and i == n - 1), is_transpose=True,
                 )
 
-        def close_sum(b):
-            empty(LISTS * b + 2)
-            add_to_sum(b, res["s", b], 0, CHUNKS, False, True)
-            leave_sum(b, 0, CHUNKS)
+        scaled, tops = {}, {}
+
+        def times_g(b, d):
+            if (b, d) == (0, 0):
+                scaled[b, d] = placed(0, [P, T], F32, "scaled00")
+            else:
+                scaled[b, d] = own([P, T], F32, f"scaled{b}{d}", f"scaled{b}{d}")
+            nc.vector.tensor_tensor(scaled[b, d][:], fetched[b][d], accs["g", b][:], ALU.mult)
+
+        def floor_at(b, d):
+            tops[b, d] = own([P, T], F32, f"top{b}{d}")
+            nc.vector.scalar_tensor_tensor(
+                out=tops[b, d][:], in0=accs["s", b][:], scalar=-1.0, in1=scaled[b, d][:], op0=ALU.mult, op1=ALU.max
+            )
+
+        def add_shift(b):
+            both = own([P, T], F32, f"shifted{b}")
+            nc.vector.scalar_tensor_tensor(
+                out=both[:], in0=accs["s", b][:], scalar=float(LISTS), in1=tops[b, 0][:], op0=ALU.mult, op1=ALU.add
+            )
+            for d, term in enumerate([tops[b, 1], tops[b, 2], both]):
+                add_to_sum(b, term, 0, CHUNKS, d == 0, d == LISTS - 1)
 
         turned = [keep.tile([P, CHUNKS, P], F32, name=f"turned{b}") for b in range(BLOCKS)]
-        ys = [keep.tile([P, T], F32, name=f"y{b}") for b in range(BLOCKS)]
         y_codes = keep.tile([P, T], U32, name="y_codes", align_bytes=64)
         y_scales = keep.tile([P, T], U8, name="y_scales", align_bytes=64)
         out_words = out_1[0].rearrange("p c r -> p (c r)").bitcast(I32)
 
-        def leave_sum(b, v0, n):
-            nc.scalar.copy(out=turned[b][:, v0 : v0 + n, :], in_=banks[b, v0][:, :n, :])
-
-        def round_pairs(src, b, v0, n):
-            if b == 0:
-                nc.gpsimd.tensor_scalar(
-                    pairs[:, v0 : v0 + n, :, b * Q : (b + 1) * Q, :].rearrange("v i u q e -> v u i q e"),
-                    src.rearrange("v i (q u e) -> v u i q e", u=2, e=2),
-                    1.0, 0.0, ALU.mult, ALU.add,
-                )
-                return
-            nc.scalar.copy(
-                out=pairs[:, v0 : v0 + n, :, b * Q : (b + 1) * Q, :],
-                in_=src.rearrange("v i (q u e) -> v i u q e", u=2, e=2),
-            )
-
-        def turn_back(b, v0, n):
+        def turn_back(b, v0, n, y, on_vector, ring):
             cols = slice(v0 * P, (v0 + n) * P)
-            bank = psum.tile([P, CHUNKS, P], F32, name="back")
+            bank = psum.tile([P, CHUNKS, P], F32, name=ring)
             for i in range(n):
                 nc.tensor.transpose(bank[:, i, :], turned[b][:, v0 + i, :], ident[:])
-            if v0 > 0:
-                nc.vector.tensor_copy(out=ys[b][:, cols], in_=bank[:, :n, :].rearrange("p i v -> p (i v)"))
+            if on_vector:
+                nc.vector.tensor_copy(out=y, in_=bank[:, :n, :].rearrange("p i v -> p (i v)"))
             else:
-                nc.scalar.copy(out=ys[b][:, cols], in_=bank[:, :n, :].rearrange("p i v -> p (i v)"))
-            nc.sync.dma_start(out=out_0[b * P : (b + 1) * P, cols], in_=ys[b][:, cols])
+                nc.scalar.copy(out=y, in_=bank[:, :n, :].rearrange("p i v -> p (i v)"))
+            nc.sync.dma_start(out=out_0[b * P : (b + 1) * P, cols], in_=y)
 
         def planes(i):
             cols = slice(i * P, (i + 1) * P)
-            bank = psum.tile([P, 2, P], F32, name="acc")
+            bank = psum.tile([P, 2, P], F32, name="back" if i < 2 else "acc")
             for u in range(2):
                 words = pairs[:, i, u, :, :].rearrange("v l e -> v (l e)").bitcast(F32)
                 nc.tensor.transpose(bank[:, u, :], words, ident[:])
@@ -237,82 +220,107 @@ def tile_picked_wfilmg_relu_lo_kernel(
                 in_=grouped[:].rearrange("p v t -> p (v t)"),
             )
 
-        cast(0)
-        multiply(0)
-        cast(1)
-        multiply(1)
-        empty(0)
-        fetched = keep.tile([P, T], F32, name="fetched", tag="grp1", align_bytes=64)
-        nc.vector.tensor_copy(fetched[:], res["h", 0][:].indirect(lists[0][:]))
-        empty(1)
-        cast(2)
-        gather(0, 1, 0, CHUNKS, keep.tile([P, T], F32, name="a01", align_bytes=64))
-        multiply(2)
-        cast(3)
-        cast(4)
-        gather(0, 2, 0, CHUNKS, after_cast("a02", 2, 0))
-        multiply(3)
-        multiply(4)
-        empty(3)
-        empty(4)
-        scaled[0, 0, 0] = after_cast("a00", 4, 0)
-        nc.vector.tensor_tensor(scaled[0, 0, 0][:], fetched[:], res["g", 0][:], ALU.mult)
-        cast(5)
-        cast(6)
-        floor_at(0, 1, 0, CHUNKS, after_cast("m01", 4, 1))
-        add_to_sum(0, tops[0, 1, 0], 0, CHUNKS, True, False)
-        floor_at(0, 2, 0, CHUNKS, after_cast("m02", 4, 3))
-        add_to_sum(0, tops[0, 2, 0], 0, CHUNKS, False, False)
-        floor_at(0, 0, 0, CHUNKS, keep.tile([P, T], F32, name="m00", align_bytes=64))
-        add_to_sum(0, tops[0, 0, 0], 0, CHUNKS, False, False)
-        cast(7)
-        close_sum(0)
-        for b in range(1, LAST):
-            shift, h_next, g_next = LISTS * b + 2, LISTS * b + 3, LISTS * b + 4
-            gather(b, 0, 0, CHUNKS, keep.tile([P, T], F32, name=f"a{b}0", align_bytes=64))
-            multiply(shift)
-            multiply(h_next)
-            wide = tied.tile([P, SLOT // 2], F32, name=f"a{b}1", offset=(PLACES * h_next - 1) * SLOT, align_bytes=64)
-            gather(b, 1, 0, CHUNKS, wide)
-            multiply(g_next)
-            if b == LAST - 1:
-                cast(final)
-            empty(h_next)
-            empty(g_next)
-            gather(b, 2, 0, CHUNKS, after_cast(f"a{b}2", g_next, 0))
-            if b == LAST - 1:
-                multiply(g_next + 1)
-                empty(g_next + 1)
-                tiles = [after_cast(f"m{b}{d}", g_next + 1, d) for d in range(LISTS)]
-            else:
-                cast(g_next + 1)
-                cast(g_next + 2)
-                cast(g_next + 3)
-                tiles = [after_cast(f"m{b}0", g_next, 1), after_cast(f"m{b}1", g_next, 3)]
-                tiles.append(keep.tile([P, T], F32, name=f"m{b}2", align_bytes=64))
-            for d in range(LISTS):
-                floor_at(b, d, 0, CHUNKS, tiles[d])
-                add_to_sum(b, tops[b, d, 0], 0, CHUNKS, d == 0, False)
-            close_sum(b)
-        pairs = keep.tile([P, CHUNKS, 2, P, 2], BF16, name="pairs", tag="grp11", align_bytes=64)
+        GROUPED = [P, PASSES, P, PACK]
+        CODES = [P, PASSES, P]
+
+        cast("h", 0, "sv", own(GROUPED, BF16, "grp_h0")[:])
+        multiply("h", 0, own(CODES, U32, "cod_h0"), True)
+        cast("g", 0, "sv", own(GROUPED, BF16, "grp_g0")[:])
+        multiply("g", 0, own(CODES, U32, "cod_g0"))
+        fetch(0, [(0, CHUNKS)])
+        cast("s", 0, "vv", own(GROUPED, BF16, "grp_s0")[:])
+        multiply("s", 0, own(CODES, U32, "cod_s0"))
+        cast("h", 1, "vv", placed(1 * KIB, GROUPED, BF16, "grp_h1")[:])
+        multiply("h", 1, own(CODES, U32, "cod_h1"))
+        fetch(1, [(0, CHUNKS)])
+        times_g(0, 0)
+
+        cast_on_gpsimd("g", 1, placed(2 * KIB, GROUPED, BF16, "grp_g1")[:])
+        cast_on_gpsimd("s", 1, own(GROUPED, BF16, "grp_s1")[:])
+        times_g(0, 1)
+        floor_at(0, 0)
+        times_g(0, 2)
+        floor_at(0, 1)
+        multiply("g", 1, own(CODES, U32, "cod_g1", "fetched02"))
+        multiply("s", 1, own(CODES, U32, "cod_s1"))
+        cast_on_gpsimd("h", 2, placed(3 * KIB, GROUPED, BF16, "grp_h2")[:])
+        floor_at(0, 2)
+        add_shift(0)
+        times_g(1, 0)
+        multiply("h", 2, own(CODES, U32, "cod_h2", "top00"))
+        cast("h", 3, "ss", placed(8 * KIB, GROUPED, BF16, "grp_h3")[:])
+        nc.scalar.copy(out=turned[0][:], in_=banks[0, 0][:])
+        turn_back(0, 0, CHUNKS, own([P, T], F32, "y0")[:], False, "back")
+        fetch(2, [(0, CHUNKS)])
+
+        cast_on_gpsimd("g", 2, placed(2 * KIB, GROUPED, BF16, "grp_g2")[:])
+        cast_on_gpsimd("s", 2, placed(4 * KIB, GROUPED, BF16, "grp_s2")[:])
+        times_g(1, 1)
+        floor_at(1, 0)
+        times_g(1, 2)
+        floor_at(1, 1)
+        floor_at(1, 2)
+        multiply("g", 2, own(CODES, U32, "cod_g2", "scaled11"))
+        multiply("h", 3, own(CODES, U32, "cod_h3", "scaled12"))
+        multiply("s", 2, own(CODES, U32, "cod_s2"))
+        add_shift(1)
+        nc.scalar.copy(out=turned[1][:], in_=banks[1, 0][:])
+        fetch(3, PIECES)
+
+        cast_on_gpsimd("g", 3, placed(7 * KIB, GROUPED, BF16, "grp_g3")[:])
+        cast_on_gpsimd("s", 3, placed(9 * KIB, GROUPED, BF16, "grp_s3")[:])
+        for d in range(LISTS):
+            times_g(2, d)
+        multiply("g", 3, own(CODES, U32, "cod_g3", "fetched21"))
+        multiply("s", 3, own(CODES, U32, "cod_s3"))
+        for d in range(LISTS):
+            floor_at(2, d)
+        add_shift(2)
+        nc.scalar.copy(out=turned[2][:], in_=banks[2, 0][:])
+        pairs = placed(5 * KIB, [P, CHUNKS, 2, P, 2], BF16, "pairs")
         for b in range(LAST):
-            round_pairs(turned[b][:], b, 0, CHUNKS)
-            turn_back(b, 0, CHUNKS)
-        for v0, n in ((0, 2), (2, 1), (3, 1)):
-            for d in range(LISTS):
-                gather(LAST, d, v0, n, keep.tile([P, T], F32, name=f"a{LAST}{d}{v0}", tag=f"a{d}", align_bytes=64))
-            add_to_sum(LAST, res["s", LAST][:, v0 * P :], v0, n, True, False)
-            for d in range(LISTS):
-                floor_at(LAST, d, v0, n, keep.tile([P, n * P], F32, name=f"m{LAST}{d}{v0}", align_bytes=64))
-                add_to_sum(LAST, tops[LAST, d, v0], v0, n, False, d == LISTS - 1)
-            round_pairs(banks[LAST, v0][:, :n, :], LAST, v0, n)
-            leave_sum(LAST, v0, n)
-            for i in range(v0, v0 + n):
-                planes(i)
-            turn_back(LAST, v0, n)
-            if v0 != 2:
-                both = slice((v0 + n - 2) * P, (v0 + n) * P)
-                nc.sync.dma_start(out=out_words[:, both], in_=y_codes[:, both].bitcast(I32))
+            nc.gpsimd.tensor_scalar(
+                pairs[:, :, :, b * Q : (b + 1) * Q, :].rearrange("v i u q e -> v u i q e"),
+                turned[b][:].rearrange("v i (q u e) -> v u i q e", u=2, e=2),
+                1.0, 0.0, ALU.mult, ALU.add,
+            )
+        for v0, n in PIECES:
+            cols = slice(v0 * P, (v0 + n) * P)
+            wide = [P, LISTS, n * P]
+            times = own(wide, F32, f"scaled{LAST}{v0}")
+            most = own(wide, F32, f"tops{LAST}{v0}")
+            both = own([P, n * P], F32, f"shifted{LAST}{v0}")
+            nc.vector.tensor_tensor(
+                times[:], fetched[LAST, v0][:], accs["g", LAST][:, cols].unsqueeze(1).to_broadcast(wide), ALU.mult
+            )
+            nc.vector.scalar_tensor_tensor(
+                out=most[:], in0=accs["s", LAST][:, cols].unsqueeze(1).to_broadcast(wide), scalar=-1.0,
+                in1=times[:], op0=ALU.mult, op1=ALU.max,
+            )
+            nc.vector.scalar_tensor_tensor(
+                out=both[:], in0=accs["s", LAST][:, cols], scalar=float(LISTS), in1=most[:, 0, :],
+                op0=ALU.mult, op1=ALU.add,
+            )
+            for d, term in enumerate([most[:, 1, :], most[:, 2, :], both[:]]):
+                add_to_sum(LAST, term, v0, n, d == 0, d == LISTS - 1)
+        y_last = own([P, T], F32, "y3")
+        for v0, n in PIECES:
+            nc.scalar.copy(
+                out=pairs[:, v0 : v0 + n, :, LAST * Q :, :],
+                in_=banks[LAST, v0][:, :n, :].rearrange("v i (q u e) -> v i u q e", u=2, e=2),
+            )
+            if v0 == 0:
+                turn_back(1, 0, CHUNKS, own([P, T], F32, "y1", f"tops{LAST}0")[:], False, "back")
+        for v0, n in PIECES:
+            nc.vector.tensor_copy(out=turned[LAST][:, v0 : v0 + n, :], in_=banks[LAST, v0][:, :n, :])
+        turn_back(LAST - 1, 0, CHUNKS, own([P, T], F32, "y2", f"scaled{LAST}{LAST}")[:], True, "sum")
+        for i in range(CHUNKS):
+            planes(i)
+            if i % 2 == 1:
+                two = slice((i - 1) * P, (i + 1) * P)
+                nc.sync.dma_start(out=out_words[:, two], in_=y_codes[:, two].bitcast(I32))
+        for v0 in (0, 2):
+            turn_back(LAST, v0, 2, y_last[:, v0 * P : (v0 + 2) * P], False, "sum" if v0 == 0 else "shift")
         for q in range(4):
             eng = nc.sync if q % 2 == 0 else nc.scalar
             eng.dma_start(

@@ -108,9 +108,12 @@ def tile_picked_wfilmg_relu_lo_kernel(
 
         def cast_on_gpsimd(kind, b, grouped):
             grp[kind, b] = grouped
-            nc.gpsimd.tensor_scalar(
-                grouped, raw[kind, b][:].rearrange("p z j m -> p z m j"), 1.0, 0.0, ALU.mult, ALU.add
-            )
+            for z in range(PASSES):
+                nc.gpsimd.tensor_scalar(
+                    grouped[:, z, :, :].rearrange("p (c i) j -> p c j i", i=2),
+                    raw[kind, b][:, z, :, :].rearrange("p j (c i) -> p c j i", i=2),
+                    1.0, 0.0, ALU.mult, ALU.add,
+                )
 
         def multiply(kind, b, codes, by_pass=False):
             scales = keep.tile([P, PASSES, P], U8, name=f"scl_{kind}{b}", align_bytes=64)

@@ -21,13 +21,18 @@ P = 128
 PACK = 4
 PASSES = K // (P * PACK)
 BLOCKS = N // P
+LAST = BLOCKS - 1
 CHUNKS = T // P
 LISTS = 3
-SPARE = 16
-Q = P // PACK
-LAST = BLOCKS - 1
-KIB = 1024
+LIST_ROWS = 16
+QUADRANTS = 4
+WORDS_A_BLOCK = P // PACK
+SPARE = LIST_ROWS
 PIECES = ((0, 2), (2, 1), (3, 1))
+PAIR = 2
+KIB = 1024
+ROUNDED = [P, PASSES, P, PACK]
+CODES = [P, PASSES, P]
 
 
 def tile_picked_wfilmg_relu_lo_kernel(
@@ -39,7 +44,13 @@ def tile_picked_wfilmg_relu_lo_kernel(
         tied = ctx.enter_context(tc.tile_pool(name="tied", bufs=1))
         psum = ctx.enter_context(tc.psum_pool(name="psum", bufs=2))
 
-        lists = [keep.tile([P, T // 16], U16, name=f"list{d}") for d in range(LISTS)]
+        def own(shape, dtype, name, after=None):
+            return keep.tile(shape, dtype, name=name, tag=after or name, align_bytes=64)
+
+        def placed(kib, shape, dtype, name):
+            return tied.tile(shape, dtype, name=name, offset=kib * KIB, align_bytes=64)
+
+        lists = [keep.tile([P, T // LIST_ROWS], U16, name=f"list{d}") for d in range(LISTS)]
         xw = keep.tile([P, PASSES, 2 * T], U8, name="xw", align_bytes=64)
         xs = keep.tile([P, PASSES, T], U8, name="xs", align_bytes=64)
         xs_in = keep.tile([P, PASSES, T], U8, name="xs_in", align_bytes=64)
@@ -52,31 +63,24 @@ def tile_picked_wfilmg_relu_lo_kernel(
         raw = {}
 
         def load_w(kind, b):
-            both = keep.tile([P, PASSES, PACK, P], F32, name=f"raw_{kind}{b}", align_bytes=64)
-            raw[kind, b] = both
+            raw[kind, b] = keep.tile([P, PASSES, PACK, P], F32, name=f"raw_{kind}{b}", align_bytes=64)
             for z in range(PASSES):
                 rows = weights[kind][z * P * PACK : (z + 1) * P * PACK, b * P : (b + 1) * P]
-                nc.sync.dma_start(out=both[:, z, :, :], in_=rows.rearrange("(p j) m -> p j m", j=PACK))
+                nc.sync.dma_start(out=raw[kind, b][:, z, :, :], in_=rows.rearrange("(p j) m -> p j m", j=PACK))
 
-        for q in range(4):
+        for q in range(QUADRANTS):
             nc.sync.dma_start(
                 out=xs_in[32 * q : 32 * q + 4, :, :].bitcast(I32),
                 in_=x_scales[:, 4 * q : 4 * q + 4, :].rearrange("z q c -> q z c").bitcast(I32),
             )
         load_w("h", 0)
         nc.sync.dma_start(out=xw[:], in_=x_words.rearrange("z p c -> p z c"))
-        load_w("g", 0)
-        nc.sync.dma_start(lists[0][:], pos1)
-        load_w("s", 0)
-        load_w("h", 1)
-        nc.sync.dma_start(lists[1][:], pos2)
-        nc.sync.dma_start(lists[2][:], pos3)
-        for b in range(1, BLOCKS):
-            load_w("g", b)
-            load_w("s", b)
-            if b < LAST:
-                load_w("h", b + 1)
-        for q in range(4):
+        for d, (pos, kind, b) in enumerate(((pos1, "g", 0), (pos2, "s", 0), (pos3, "h", 1))):
+            load_w(kind, b)
+            nc.sync.dma_start(lists[d][:], pos)
+        for kind, b in (("g", 1), ("s", 1), ("h", 2), ("h", 3), ("g", 2), ("s", 2), ("g", 3), ("s", 3)):
+            load_w(kind, b)
+        for q in range(QUADRANTS):
             nc.vector.tensor_copy(
                 out=xs[32 * q : 32 * q + 4, :, :].bitcast(I32), in_=xs_in[32 * q : 32 * q + 4, :, :].bitcast(I32)
             )
@@ -88,53 +92,40 @@ def tile_picked_wfilmg_relu_lo_kernel(
         for b in range(1, BLOCKS):
             nc.gpsimd.memset(hs[b][:, T:], 0.0)
 
-        grp, accs, banks = {}, {}, {}
+        rounded, accs, sums = {}, {}, {}
+        fetched, scaled, tops = {}, {}, {}
 
-        def placed(offset, shape, dtype, name):
-            return tied.tile(shape, dtype, name=name, offset=offset, align_bytes=64)
-
-        def own(shape, dtype, name, tag=None):
-            return keep.tile(shape, dtype, name=name, tag=tag or name, align_bytes=64)
-
-        def cast(kind, b, engines, grouped):
-            grp[kind, b] = grouped
-            for z, eng in enumerate(engines):
-                dst = grouped[:, z, :, :].rearrange("p (c i) j -> p c j i", i=2)
-                src = raw[kind, b][:, z, :, :].rearrange("p j (c i) -> p c j i", i=2)
-                if eng == "v":
+        def cast(kind, b, engines, tile):
+            rounded[kind, b] = tile
+            for z, engine in enumerate(engines):
+                dst = tile[:, z, :, :].rearrange("p (c i) j -> p c j i", i=PAIR)
+                src = raw[kind, b][:, z, :, :].rearrange("p j (c i) -> p c j i", i=PAIR)
+                if engine == "vector":
                     nc.vector.tensor_copy(out=dst, in_=src)
-                else:
+                elif engine == "scalar":
                     nc.scalar.copy(out=dst, in_=src)
-
-        def cast_on_gpsimd(kind, b, grouped):
-            grp[kind, b] = grouped
-            for z in range(PASSES):
-                nc.gpsimd.tensor_scalar(
-                    grouped[:, z, :, :].rearrange("p (c i) j -> p c j i", i=2),
-                    raw[kind, b][:, z, :, :].rearrange("p j (c i) -> p c j i", i=2),
-                    1.0, 0.0, ALU.mult, ALU.add,
-                )
+                else:
+                    nc.gpsimd.tensor_scalar(dst, src, 1.0, 0.0, ALU.mult, ALU.add)
 
         def multiply(kind, b, codes, by_pass=False):
-            scales = keep.tile([P, PASSES, P], U8, name=f"scl_{kind}{b}", align_bytes=64)
+            scales = keep.tile(CODES, U8, name=f"scl_{kind}{b}", align_bytes=64)
             if by_pass:
                 for z in range(PASSES):
                     nc.vector.quantize_mx(
                         out=codes[:, z, :].bitcast(FP8X4),
                         scales=scales[:, z, :],
-                        in_=grp[kind, b][:, z, :, :].rearrange("p m j -> p (m j)"),
+                        in_=rounded[kind, b][:, z, :, :].rearrange("p m j -> p (m j)"),
                     )
             else:
                 nc.vector.quantize_mx(
                     out=codes[:].rearrange("p z m -> p (z m)").bitcast(FP8X4),
                     scales=scales[:].rearrange("p z m -> p (z m)"),
-                    in_=grp[kind, b].rearrange("p z m j -> p (z m j)"),
+                    in_=rounded[kind, b].rearrange("p z m j -> p (z m j)"),
                 )
-            acc = psum.tile([P, T], F32, name="shift" if kind == "s" else "acc")
-            accs[kind, b] = acc
+            accs[kind, b] = psum.tile([P, T], F32, name="shift" if kind == "s" else "acc")
             for z in range(PASSES):
                 nc.tensor.matmul_mx(
-                    out=acc[:],
+                    out=accs[kind, b][:],
                     lhsT=codes[:, z, :].bitcast(FP8X4),
                     lhsT_scale=scales[:, z, :],
                     rhs=xw[:, z, :].bitcast(FP4X4),
@@ -143,39 +134,36 @@ def tile_picked_wfilmg_relu_lo_kernel(
                     stop=(z == PASSES - 1),
                 )
 
-        fetched = {}
+        def gather(b, d, i0, n, out):
+            offsets = lists[d][:, i0 * P // LIST_ROWS : (i0 + n) * P // LIST_ROWS]
+            nc.scalar.activation(out=out, in_=hs[b][:].indirect(offsets), func=COPY)
 
-        def fetch(b, pieces):
+        def fetch(b):
             nc.scalar.copy(out=hs[b][:, :T], in_=accs["h", b][:])
-            for v0, n in pieces:
-                if n == CHUNKS:
-                    rows = [own([P, T], F32, f"fetched{b}{d}", f"fetched{b}{d}")[:] for d in range(LISTS)]
-                    fetched[b] = rows
-                else:
-                    fetched[b, v0] = own([P, LISTS, n * P], F32, f"fetched{b}{v0}")
-                    rows = [fetched[b, v0][:, d, :] for d in range(LISTS)]
+            for d in range(LISTS):
+                fetched[b, d] = own([P, T], F32, f"fetched{b}{d}")
+            for d in range(LISTS):
+                gather(b, d, 0, CHUNKS, fetched[b, d][:])
+
+        def fetch_last():
+            nc.scalar.copy(out=hs[LAST][:, :T], in_=accs["h", LAST][:])
+            for i0, n in PIECES:
+                fetched[LAST, i0] = own([P, LISTS, n * P], F32, f"fetched{LAST}{i0}")
                 for d in range(LISTS):
-                    nc.scalar.activation(
-                        out=rows[d], in_=hs[b][:].indirect(lists[d][:, v0 * 8 : (v0 + n) * 8]), func=COPY
+                    gather(LAST, d, i0, n, fetched[LAST, i0][:, d, :])
+
+        def add_up(b, i0, n, terms, ring):
+            sums[b, i0] = psum.tile([P, CHUNKS, P], F32, name=ring)
+            for t, term in enumerate(terms):
+                for i in range(n):
+                    nc.tensor.matmul(
+                        sums[b, i0][:, i, :], lhsT=term[:, i * P : (i + 1) * P], rhs=ident[:],
+                        start=(t == 0 and i == 0), stop=(t == len(terms) - 1 and i == n - 1), is_transpose=True,
                     )
 
-        def add_to_sum(b, term, v0, n, first, last):
-            if first:
-                banks[b, v0] = psum.tile([P, CHUNKS, P], F32, name={0: "sum", 2: "acc", 3: "shift"}[v0])
-            for i in range(n):
-                nc.tensor.matmul(
-                    banks[b, v0][:, i, :], lhsT=term[:, i * P : (i + 1) * P], rhs=ident[:],
-                    start=(first and i == 0), stop=(last and i == n - 1), is_transpose=True,
-                )
-
-        scaled, tops = {}, {}
-
-        def times_g(b, d):
-            if (b, d) == (0, 0):
-                scaled[b, d] = placed(0, [P, T], F32, "scaled00")
-            else:
-                scaled[b, d] = own([P, T], F32, f"scaled{b}{d}", f"scaled{b}{d}")
-            nc.vector.tensor_tensor(scaled[b, d][:], fetched[b][d], accs["g", b][:], ALU.mult)
+        def times_g(b, d, tile=None):
+            scaled[b, d] = own([P, T], F32, f"scaled{b}{d}") if tile is None else tile
+            nc.vector.tensor_tensor(scaled[b, d][:], fetched[b, d][:], accs["g", b][:], ALU.mult)
 
         def floor_at(b, d):
             tops[b, d] = own([P, T], F32, f"top{b}{d}")
@@ -183,33 +171,31 @@ def tile_picked_wfilmg_relu_lo_kernel(
                 out=tops[b, d][:], in0=accs["s", b][:], scalar=-1.0, in1=scaled[b, d][:], op0=ALU.mult, op1=ALU.max
             )
 
-        def add_shift(b):
-            both = own([P, T], F32, f"shifted{b}")
+        def close(b):
+            shifted = own([P, T], F32, f"shifted{b}")
             nc.vector.scalar_tensor_tensor(
-                out=both[:], in0=accs["s", b][:], scalar=float(LISTS), in1=tops[b, 0][:], op0=ALU.mult, op1=ALU.add
+                out=shifted[:], in0=accs["s", b][:], scalar=float(LISTS), in1=tops[b, 0][:], op0=ALU.mult, op1=ALU.add
             )
-            for d, term in enumerate([tops[b, 1], tops[b, 2], both]):
-                add_to_sum(b, term, 0, CHUNKS, d == 0, d == LISTS - 1)
+            add_up(b, 0, CHUNKS, [tops[b, 1], tops[b, 2], shifted], "sum")
 
         turned = [keep.tile([P, CHUNKS, P], F32, name=f"turned{b}") for b in range(BLOCKS)]
         y_codes = keep.tile([P, T], U32, name="y_codes", align_bytes=64)
         y_scales = keep.tile([P, T], U8, name="y_scales", align_bytes=64)
         out_words = out_1[0].rearrange("p c r -> p (c r)").bitcast(I32)
 
-        def turn_back(b, v0, n, y, on_vector, ring):
-            cols = slice(v0 * P, (v0 + n) * P)
+        def store_rows(b, i0, n, y, engine, ring):
             bank = psum.tile([P, CHUNKS, P], F32, name=ring)
             for i in range(n):
-                nc.tensor.transpose(bank[:, i, :], turned[b][:, v0 + i, :], ident[:])
-            if on_vector:
+                nc.tensor.transpose(bank[:, i, :], turned[b][:, i0 + i, :], ident[:])
+            if engine == "vector":
                 nc.vector.tensor_copy(out=y, in_=bank[:, :n, :].rearrange("p i v -> p (i v)"))
             else:
                 nc.scalar.copy(out=y, in_=bank[:, :n, :].rearrange("p i v -> p (i v)"))
-            nc.sync.dma_start(out=out_0[b * P : (b + 1) * P, cols], in_=y)
+            nc.sync.dma_start(out=out_0[b * P : (b + 1) * P, i0 * P : (i0 + n) * P], in_=y)
 
-        def planes(i):
+        def planes(i, ring):
             cols = slice(i * P, (i + 1) * P)
-            bank = psum.tile([P, 2, P], F32, name="back" if i < 2 else "acc")
+            bank = psum.tile([P, 2, P], F32, name=ring)
             for u in range(2):
                 words = pairs[:, i, u, :, :].rearrange("v l e -> v (l e)").bitcast(F32)
                 nc.tensor.transpose(bank[:, u, :], words, ident[:])
@@ -223,110 +209,112 @@ def tile_picked_wfilmg_relu_lo_kernel(
                 in_=grouped[:].rearrange("p v t -> p (v t)"),
             )
 
-        GROUPED = [P, PASSES, P, PACK]
-        CODES = [P, PASSES, P]
+        on_gpsimd = ("gpsimd", "gpsimd")
 
-        cast("h", 0, "sv", own(GROUPED, BF16, "grp_h0")[:])
-        multiply("h", 0, own(CODES, U32, "cod_h0"), True)
-        cast("g", 0, "sv", own(GROUPED, BF16, "grp_g0")[:])
+        cast("h", 0, ("scalar", "vector"), own(ROUNDED, BF16, "grp_h0")[:])
+        multiply("h", 0, own(CODES, U32, "cod_h0"), by_pass=True)
+        cast("g", 0, ("scalar", "vector"), own(ROUNDED, BF16, "grp_g0")[:])
         multiply("g", 0, own(CODES, U32, "cod_g0"))
-        fetch(0, [(0, CHUNKS)])
-        cast("s", 0, "vv", own(GROUPED, BF16, "grp_s0")[:])
+        fetch(0)
+        cast("s", 0, ("vector", "vector"), own(ROUNDED, BF16, "grp_s0")[:])
         multiply("s", 0, own(CODES, U32, "cod_s0"))
-        cast("h", 1, "vv", placed(1 * KIB, GROUPED, BF16, "grp_h1")[:])
+        cast("h", 1, ("vector", "vector"), placed(1, ROUNDED, BF16, "grp_h1")[:])
         multiply("h", 1, own(CODES, U32, "cod_h1"))
-        fetch(1, [(0, CHUNKS)])
-        times_g(0, 0)
+        fetch(1)
 
-        cast_on_gpsimd("g", 1, placed(2 * KIB, GROUPED, BF16, "grp_g1")[:])
-        cast_on_gpsimd("s", 1, own(GROUPED, BF16, "grp_s1")[:])
+        times_g(0, 0, placed(0, [P, T], F32, "scaled00"))
+        cast("g", 1, on_gpsimd, placed(2, ROUNDED, BF16, "grp_g1")[:])
+        cast("s", 1, on_gpsimd, own(ROUNDED, BF16, "grp_s1")[:])
         times_g(0, 1)
         floor_at(0, 0)
         times_g(0, 2)
         floor_at(0, 1)
-        multiply("g", 1, own(CODES, U32, "cod_g1", "fetched02"))
+        multiply("g", 1, own(CODES, U32, "cod_g1", after="fetched02"))
         multiply("s", 1, own(CODES, U32, "cod_s1"))
-        cast_on_gpsimd("h", 2, placed(3 * KIB, GROUPED, BF16, "grp_h2")[:])
+        cast("h", 2, on_gpsimd, placed(3, ROUNDED, BF16, "grp_h2")[:])
         floor_at(0, 2)
-        add_shift(0)
+        close(0)
         times_g(1, 0)
-        multiply("h", 2, own(CODES, U32, "cod_h2", "top00"))
-        cast("h", 3, "ss", placed(8 * KIB, GROUPED, BF16, "grp_h3")[:])
-        nc.scalar.copy(out=turned[0][:], in_=banks[0, 0][:])
-        turn_back(0, 0, CHUNKS, own([P, T], F32, "y0")[:], False, "back")
-        fetch(2, [(0, CHUNKS)])
+        multiply("h", 2, own(CODES, U32, "cod_h2", after="top00"))
+        cast("h", 3, ("scalar", "scalar"), placed(8, ROUNDED, BF16, "grp_h3")[:])
+        nc.scalar.copy(out=turned[0][:], in_=sums[0, 0][:])
+        store_rows(0, 0, CHUNKS, own([P, T], F32, "y0")[:], "scalar", "back")
+        fetch(2)
 
-        cast_on_gpsimd("g", 2, placed(2 * KIB, GROUPED, BF16, "grp_g2")[:])
-        cast_on_gpsimd("s", 2, placed(4 * KIB, GROUPED, BF16, "grp_s2")[:])
+        cast("g", 2, on_gpsimd, placed(2, ROUNDED, BF16, "grp_g2")[:])
+        cast("s", 2, on_gpsimd, placed(4, ROUNDED, BF16, "grp_s2")[:])
         times_g(1, 1)
         floor_at(1, 0)
         times_g(1, 2)
         floor_at(1, 1)
         floor_at(1, 2)
-        multiply("g", 2, own(CODES, U32, "cod_g2", "scaled11"))
-        multiply("h", 3, own(CODES, U32, "cod_h3", "scaled12"))
+        multiply("g", 2, own(CODES, U32, "cod_g2", after="scaled11"))
+        multiply("h", 3, own(CODES, U32, "cod_h3", after="scaled12"))
         multiply("s", 2, own(CODES, U32, "cod_s2"))
-        add_shift(1)
-        nc.scalar.copy(out=turned[1][:], in_=banks[1, 0][:])
-        fetch(3, PIECES)
+        close(1)
+        nc.scalar.copy(out=turned[1][:], in_=sums[1, 0][:])
+        fetch_last()
 
-        cast_on_gpsimd("g", 3, placed(7 * KIB, GROUPED, BF16, "grp_g3")[:])
-        cast_on_gpsimd("s", 3, placed(9 * KIB, GROUPED, BF16, "grp_s3")[:])
+        cast("g", 3, on_gpsimd, placed(7, ROUNDED, BF16, "grp_g3")[:])
+        cast("s", 3, on_gpsimd, placed(9, ROUNDED, BF16, "grp_s3")[:])
         for d in range(LISTS):
             times_g(2, d)
-        multiply("g", 3, own(CODES, U32, "cod_g3", "fetched21"))
+        multiply("g", 3, own(CODES, U32, "cod_g3", after="fetched21"))
         multiply("s", 3, own(CODES, U32, "cod_s3"))
         for d in range(LISTS):
             floor_at(2, d)
-        add_shift(2)
-        nc.scalar.copy(out=turned[2][:], in_=banks[2, 0][:])
-        pairs = placed(5 * KIB, [P, CHUNKS, 2, P, 2], BF16, "pairs")
+        close(2)
+        nc.scalar.copy(out=turned[2][:], in_=sums[2, 0][:])
+
+        pairs = placed(5, [P, CHUNKS, 2, P, 2], BF16, "pairs")
         for b in range(LAST):
             nc.gpsimd.tensor_scalar(
-                pairs[:, :, :, b * Q : (b + 1) * Q, :].rearrange("v i u q e -> v u i q e"),
-                turned[b][:].rearrange("v i (q u e) -> v u i q e", u=2, e=2),
+                pairs[:, :, :, b * WORDS_A_BLOCK : (b + 1) * WORDS_A_BLOCK, :].rearrange("v i u l e -> v u i l e"),
+                turned[b][:].rearrange("v i (l u e) -> v u i l e", u=2, e=2),
                 1.0, 0.0, ALU.mult, ALU.add,
             )
-        for v0, n in PIECES:
-            cols = slice(v0 * P, (v0 + n) * P)
+
+        for (i0, n), ring in zip(PIECES, ("sum", "acc", "shift")):
+            cols = slice(i0 * P, (i0 + n) * P)
             wide = [P, LISTS, n * P]
-            times = own(wide, F32, f"scaled{LAST}{v0}")
-            most = own(wide, F32, f"tops{LAST}{v0}")
-            both = own([P, n * P], F32, f"shifted{LAST}{v0}")
+            piece_scaled = own(wide, F32, f"scaled{LAST}{i0}")
+            piece_tops = own(wide, F32, f"tops{LAST}{i0}")
+            piece_shifted = own([P, n * P], F32, f"shifted{LAST}{i0}")
             nc.vector.tensor_tensor(
-                times[:], fetched[LAST, v0][:], accs["g", LAST][:, cols].unsqueeze(1).to_broadcast(wide), ALU.mult
+                piece_scaled[:], fetched[LAST, i0][:], accs["g", LAST][:, cols].unsqueeze(1).to_broadcast(wide),
+                ALU.mult,
             )
             nc.vector.scalar_tensor_tensor(
-                out=most[:], in0=accs["s", LAST][:, cols].unsqueeze(1).to_broadcast(wide), scalar=-1.0,
-                in1=times[:], op0=ALU.mult, op1=ALU.max,
+                out=piece_tops[:], in0=accs["s", LAST][:, cols].unsqueeze(1).to_broadcast(wide), scalar=-1.0,
+                in1=piece_scaled[:], op0=ALU.mult, op1=ALU.max,
             )
             nc.vector.scalar_tensor_tensor(
-                out=both[:], in0=accs["s", LAST][:, cols], scalar=float(LISTS), in1=most[:, 0, :],
+                out=piece_shifted[:], in0=accs["s", LAST][:, cols], scalar=float(LISTS), in1=piece_tops[:, 0, :],
                 op0=ALU.mult, op1=ALU.add,
             )
-            for d, term in enumerate([most[:, 1, :], most[:, 2, :], both[:]]):
-                add_to_sum(LAST, term, v0, n, d == 0, d == LISTS - 1)
+            add_up(LAST, i0, n, [piece_tops[:, 1, :], piece_tops[:, 2, :], piece_shifted[:]], ring)
+
         y_last = own([P, T], F32, "y3")
-        for v0, n in PIECES:
+        for i0, n in PIECES:
             nc.scalar.copy(
-                out=pairs[:, v0 : v0 + n, :, LAST * Q :, :],
-                in_=banks[LAST, v0][:, :n, :].rearrange("v i (q u e) -> v i u q e", u=2, e=2),
+                out=pairs[:, i0 : i0 + n, :, LAST * WORDS_A_BLOCK :, :],
+                in_=sums[LAST, i0][:, :n, :].rearrange("v i (l u e) -> v i u l e", u=2, e=2),
             )
-            if v0 == 0:
-                turn_back(1, 0, CHUNKS, own([P, T], F32, "y1", f"tops{LAST}0")[:], False, "back")
-        for v0, n in PIECES:
-            nc.vector.tensor_copy(out=turned[LAST][:, v0 : v0 + n, :], in_=banks[LAST, v0][:, :n, :])
-        turn_back(LAST - 1, 0, CHUNKS, own([P, T], F32, "y2", f"scaled{LAST}{LAST}")[:], True, "sum")
-        for i in range(CHUNKS):
-            planes(i)
+            if i0 == PIECES[0][0]:
+                store_rows(1, 0, CHUNKS, own([P, T], F32, "y1", after=f"tops{LAST}{i0}")[:], "scalar", "back")
+        for i0, n in PIECES:
+            nc.vector.tensor_copy(out=turned[LAST][:, i0 : i0 + n, :], in_=sums[LAST, i0][:, :n, :])
+        store_rows(2, 0, CHUNKS, own([P, T], F32, "y2", after=f"scaled{LAST}{PIECES[-1][0]}")[:], "vector", "sum")
+        for i, ring in enumerate(("back", "back", "acc", "acc")):
+            planes(i, ring)
             if i % 2 == 1:
-                two = slice((i - 1) * P, (i + 1) * P)
-                nc.sync.dma_start(out=out_words[:, two], in_=y_codes[:, two].bitcast(I32))
-        for v0 in (0, 2):
-            turn_back(LAST, v0, 2, y_last[:, v0 * P : (v0 + 2) * P], False, "sum" if v0 == 0 else "shift")
-        for q in range(4):
-            eng = nc.sync if q % 2 == 0 else nc.scalar
-            eng.dma_start(
+                half = slice((i - 1) * P, (i + 1) * P)
+                nc.sync.dma_start(out=out_words[:, half], in_=y_codes[:, half].bitcast(I32))
+        for i0, ring in ((0, "sum"), (2, "shift")):
+            store_rows(LAST, i0, 2, y_last[:, i0 * P : (i0 + 2) * P], "scalar", ring)
+        for q in range(QUADRANTS):
+            queue = nc.sync if q % 2 == 0 else nc.scalar
+            queue.dma_start(
                 out=out_2[0, 4 * q : 4 * q + 4, :].bitcast(I32),
                 in_=y_scales[32 * q : 32 * q + 4, :].bitcast(I32),
             )

from contextlib import ExitStack

import concourse.mybir as mybir
from concourse.masks import make_identity

K, T, N = 1024, 512, 512
FLOPS = 3 * 2 * K * T * N

F32 = mybir.dt.float32
BF16 = mybir.dt.bfloat16
I32 = mybir.dt.int32
U32 = mybir.dt.uint32
U16 = mybir.dt.uint16
U8 = mybir.dt.uint8
FP8X4 = mybir.dt.float8_e4m3fn_x4
FP4X4 = mybir.dt.float4_e2m1fn_x4
ALU = mybir.AluOpType
COPY = mybir.ActivationFunctionType.Copy

P = 128
PACK = 4
PASSES = K // (P * PACK)
BLOCKS = N // P
LAST = BLOCKS - 1
CHUNKS = T // P
LISTS = 3
LIST_ROWS = 16
QUADRANTS = 4
WORDS_A_BLOCK = P // PACK
SPARE = LIST_ROWS
PIECES = ((0, 2), (2, 1), (3, 1))
PAIR = 2
KIB = 1024
ROUNDED = [P, PASSES, P, PACK]
CODES = [P, PASSES, P]


def tile_picked_wfilmg_relu_lo_kernel(
    tc, x_words, x_scales, w1, w2, w3, pos1, pos2, pos3, out_0, out_1, out_2
):
    nc = tc.nc
    with ExitStack() as ctx:
        keep = ctx.enter_context(tc.tile_pool(name="keep", bufs=1))
        tied = ctx.enter_context(tc.tile_pool(name="tied", bufs=1))
        psum = ctx.enter_context(tc.psum_pool(name="psum", bufs=2))

        def own(shape, dtype, name, after=None):
            return keep.tile(shape, dtype, name=name, tag=after or name, align_bytes=64)

        def placed(kib, shape, dtype, name):
            return tied.tile(shape, dtype, name=name, offset=kib * KIB, align_bytes=64)

        lists = [keep.tile([P, T // LIST_ROWS], U16, name=f"list{d}") for d in range(LISTS)]
        xw = keep.tile([P, PASSES, 2 * T], U8, name="xw", align_bytes=64)
        xs = keep.tile([P, PASSES, T], U8, name="xs", align_bytes=64)
        xs_in = keep.tile([P, PASSES, T], U8, name="xs_in", align_bytes=64)
        ident = keep.tile([P, P], F32, name="ident")

        nc.vector.memset(xs[:].rearrange("p z c -> p (z c)").bitcast(I32), 0)
        make_identity(nc, ident[:])

        weights = {"h": w3, "g": w1, "s": w2}
        raw = {}

        def load_w(kind, b):
            raw[kind, b] = keep.tile([P, PASSES, PACK, P], F32, name=f"raw_{kind}{b}", align_bytes=64)
            for z in range(PASSES):
                rows = weights[kind][z * P * PACK : (z + 1) * P * PACK, b * P : (b + 1) * P]
                nc.sync.dma_start(out=raw[kind, b][:, z, :, :], in_=rows.rearrange("(p j) m -> p j m", j=PACK))

        for q in range(QUADRANTS):
            nc.sync.dma_start(
                out=xs_in[32 * q : 32 * q + 4, :, :].bitcast(I32),
                in_=x_scales[:, 4 * q : 4 * q + 4, :].rearrange("z q c -> q z c").bitcast(I32),
            )
        load_w("h", 0)
        nc.sync.dma_start(out=xw[:], in_=x_words.rearrange("z p c -> p z c"))
        for d, (pos, kind, b) in enumerate(((pos1, "g", 0), (pos2, "s", 0), (pos3, "h", 1))):
            load_w(kind, b)
            nc.sync.dma_start(lists[d][:], pos)
        for kind, b in (("g", 1), ("s", 1), ("h", 2), ("h", 3), ("g", 2), ("s", 2), ("g", 3), ("s", 3)):
            load_w(kind, b)
        for q in range(QUADRANTS):
            nc.vector.tensor_copy(
                out=xs[32 * q : 32 * q + 4, :, :].bitcast(I32), in_=xs_in[32 * q : 32 * q + 4, :, :].bitcast(I32)
            )

        hs = [keep.tile([P, T + SPARE], F32, name=f"h{b}") for b in range(BLOCKS)]
        zeros = keep.tile([P, SPARE], F32, name="zeros")
        nc.vector.memset(zeros[:], 0.0)
        nc.scalar.activation(out=hs[0][:, T:], in_=zeros[:], func=COPY)
        for b in range(1, BLOCKS):
            nc.gpsimd.memset(hs[b][:, T:], 0.0)

        rounded, accs, sums = {}, {}, {}
        fetched, scaled, tops = {}, {}, {}

        def cast(kind, b, engines, tile):
            rounded[kind, b] = tile
            for z, engine in enumerate(engines):
                dst = tile[:, z, :, :].rearrange("p (c i) j -> p c j i", i=PAIR)
                src = raw[kind, b][:, z, :, :].rearrange("p j (c i) -> p c j i", i=PAIR)
                if engine == "vector":
                    nc.vector.tensor_copy(out=dst, in_=src)
                elif engine == "scalar":
                    nc.scalar.copy(out=dst, in_=src)
                else:
                    nc.gpsimd.tensor_scalar(dst, src, 1.0, 0.0, ALU.mult, ALU.add)

        def multiply(kind, b, codes, by_pass=False):
            scales = keep.tile(CODES, U8, name=f"scl_{kind}{b}", align_bytes=64)
            if by_pass:
                for z in range(PASSES):
                    nc.vector.quantize_mx(
                        out=codes[:, z, :].bitcast(FP8X4),
                        scales=scales[:, z, :],
                        in_=rounded[kind, b][:, z, :, :].rearrange("p m j -> p (m j)"),
                    )
            else:
                nc.vector.quantize_mx(
                    out=codes[:].rearrange("p z m -> p (z m)").bitcast(FP8X4),
                    scales=scales[:].rearrange("p z m -> p (z m)"),
                    in_=rounded[kind, b].rearrange("p z m j -> p (z m j)"),
                )
            accs[kind, b] = psum.tile([P, T], F32, name="shift" if kind == "s" else "acc")
            for z in range(PASSES):
                nc.tensor.matmul_mx(
                    out=accs[kind, b][:],
                    lhsT=codes[:, z, :].bitcast(FP8X4),
                    lhsT_scale=scales[:, z, :],
                    rhs=xw[:, z, :].bitcast(FP4X4),
                    rhs_scale=xs[:, z, :],
                    start=(z == 0),
                    stop=(z == PASSES - 1),
                )

        def gather(b, d, i0, n, out):
            offsets = lists[d][:, i0 * P // LIST_ROWS : (i0 + n) * P // LIST_ROWS]
            nc.scalar.activation(out=out, in_=hs[b][:].indirect(offsets), func=COPY)

        def fetch(b):
            nc.scalar.copy(out=hs[b][:, :T], in_=accs["h", b][:])
            for d in range(LISTS):
                fetched[b, d] = own([P, T], F32, f"fetched{b}{d}")
            for d in range(LISTS):
                gather(b, d, 0, CHUNKS, fetched[b, d][:])

        def fetch_last():
            nc.scalar.copy(out=hs[LAST][:, :T], in_=accs["h", LAST][:])
            for i0, n in PIECES:
                fetched[LAST, i0] = own([P, LISTS, n * P], F32, f"fetched{LAST}{i0}")
                for d in range(LISTS):
                    gather(LAST, d, i0, n, fetched[LAST, i0][:, d, :])

        def add_up(b, i0, n, terms, ring):
            sums[b, i0] = psum.tile([P, CHUNKS, P], F32, name=ring)
            for t, term in enumerate(terms):
                for i in range(n):
                    nc.tensor.matmul(
                        sums[b, i0][:, i, :], lhsT=term[:, i * P : (i + 1) * P], rhs=ident[:],
                        start=(t == 0 and i == 0), stop=(t == len(terms) - 1 and i == n - 1), is_transpose=True,
                    )

        def times_g(b, d, tile=None):
            scaled[b, d] = own([P, T], F32, f"scaled{b}{d}") if tile is None else tile
            nc.vector.tensor_tensor(scaled[b, d][:], fetched[b, d][:], accs["g", b][:], ALU.mult)

        def floor_at(b, d):
            tops[b, d] = own([P, T], F32, f"top{b}{d}")
            nc.vector.scalar_tensor_tensor(
                out=tops[b, d][:], in0=accs["s", b][:], scalar=-1.0, in1=scaled[b, d][:], op0=ALU.mult, op1=ALU.max
            )

        def close(b):
            shifted = own([P, T], F32, f"shifted{b}")
            nc.vector.scalar_tensor_tensor(
                out=shifted[:], in0=accs["s", b][:], scalar=float(LISTS), in1=tops[b, 0][:], op0=ALU.mult, op1=ALU.add
            )
            add_up(b, 0, CHUNKS, [tops[b, 1], tops[b, 2], shifted], "sum")

        turned = [keep.tile([P, CHUNKS, P], F32, name=f"turned{b}") for b in range(BLOCKS)]
        y_codes = keep.tile([P, T], U32, name="y_codes", align_bytes=64)
        y_scales = keep.tile([P, T], U8, name="y_scales", align_bytes=64)
        out_words = out_1[0].rearrange("p c r -> p (c r)").bitcast(I32)

        def store_rows(b, i0, n, y, engine, ring):
            bank = psum.tile([P, CHUNKS, P], F32, name=ring)
            for i in range(n):
                nc.tensor.transpose(bank[:, i, :], turned[b][:, i0 + i, :], ident[:])
            if engine == "vector":
                nc.vector.tensor_copy(out=y, in_=bank[:, :n, :].rearrange("p i v -> p (i v)"))
            else:
                nc.scalar.copy(out=y, in_=bank[:, :n, :].rearrange("p i v -> p (i v)"))
            nc.sync.dma_start(out=out_0[b * P : (b + 1) * P, i0 * P : (i0 + n) * P], in_=y)

        def planes(i, ring):
            cols = slice(i * P, (i + 1) * P)
            bank = psum.tile([P, 2, P], F32, name=ring)
            for u in range(2):
                words = pairs[:, i, u, :, :].rearrange("v l e -> v (l e)").bitcast(F32)
                nc.tensor.transpose(bank[:, u, :], words, ident[:])
            grouped = keep.tile([P, P, PACK], BF16, name=f"y_grouped{i}", align_bytes=64)
            nc.scalar.copy(
                out=grouped[:].rearrange("p v (u e) -> p v u e", e=2).bitcast(F32).rearrange("p v u e -> p v (u e)"),
                in_=bank[:].rearrange("p u v -> p v u"),
            )
            nc.vector.quantize_mx(
                out=y_codes[:, cols].bitcast(FP8X4), scales=y_scales[:, cols],
                in_=grouped[:].rearrange("p v t -> p (v t)"),
            )

        on_gpsimd = ("gpsimd", "gpsimd")

        cast("h", 0, ("scalar", "vector"), own(ROUNDED, BF16, "grp_h0")[:])
        multiply("h", 0, own(CODES, U32, "cod_h0"), by_pass=True)
        cast("g", 0, ("scalar", "vector"), own(ROUNDED, BF16, "grp_g0")[:])
        multiply("g", 0, own(CODES, U32, "cod_g0"))
        fetch(0)
        cast("s", 0, ("vector", "vector"), own(ROUNDED, BF16, "grp_s0")[:])
        multiply("s", 0, own(CODES, U32, "cod_s0"))
        cast("h", 1, ("vector", "vector"), placed(1, ROUNDED, BF16, "grp_h1")[:])
        multiply("h", 1, own(CODES, U32, "cod_h1"))
        fetch(1)

        times_g(0, 0, placed(0, [P, T], F32, "scaled00"))
        cast("g", 1, on_gpsimd, placed(2, ROUNDED, BF16, "grp_g1")[:])
        cast("s", 1, on_gpsimd, own(ROUNDED, BF16, "grp_s1")[:])
        times_g(0, 1)
        floor_at(0, 0)
        times_g(0, 2)
        floor_at(0, 1)
        multiply("g", 1, own(CODES, U32, "cod_g1", after="fetched02"))
        multiply("s", 1, own(CODES, U32, "cod_s1"))
        cast("h", 2, on_gpsimd, placed(3, ROUNDED, BF16, "grp_h2")[:])
        floor_at(0, 2)
        close(0)
        times_g(1, 0)
        multiply("h", 2, own(CODES, U32, "cod_h2", after="top00"))
        cast("h", 3, ("scalar", "scalar"), placed(8, ROUNDED, BF16, "grp_h3")[:])
        nc.scalar.copy(out=turned[0][:], in_=sums[0, 0][:])
        store_rows(0, 0, CHUNKS, own([P, T], F32, "y0")[:], "scalar", "back")
        fetch(2)

        cast("g", 2, on_gpsimd, placed(2, ROUNDED, BF16, "grp_g2")[:])
        cast("s", 2, on_gpsimd, placed(4, ROUNDED, BF16, "grp_s2")[:])
        times_g(1, 1)
        floor_at(1, 0)
        times_g(1, 2)
        floor_at(1, 1)
        floor_at(1, 2)
        multiply("g", 2, own(CODES, U32, "cod_g2", after="scaled11"))
        multiply("h", 3, own(CODES, U32, "cod_h3", after="scaled12"))
        multiply("s", 2, own(CODES, U32, "cod_s2"))
        close(1)
        nc.scalar.copy(out=turned[1][:], in_=sums[1, 0][:])
        fetch_last()

        cast("g", 3, on_gpsimd, placed(7, ROUNDED, BF16, "grp_g3")[:])
        cast("s", 3, on_gpsimd, placed(9, ROUNDED, BF16, "grp_s3")[:])
        for d in range(LISTS):
            times_g(2, d)
        multiply("g", 3, own(CODES, U32, "cod_g3", after="fetched21"))
        multiply("s", 3, own(CODES, U32, "cod_s3"))
        for d in range(LISTS):
            floor_at(2, d)
        close(2)
        nc.scalar.copy(out=turned[2][:], in_=sums[2, 0][:])

        pairs = placed(5, [P, CHUNKS, 2, P, 2], BF16, "pairs")
        for b in range(LAST):
            nc.gpsimd.tensor_scalar(
                pairs[:, :, :, b * WORDS_A_BLOCK : (b + 1) * WORDS_A_BLOCK, :].rearrange("v i u l e -> v u i l e"),
                turned[b][:].rearrange("v i (l u e) -> v u i l e", u=2, e=2),
                1.0, 0.0, ALU.mult, ALU.add,
            )

        for (i0, n), ring in zip(PIECES, ("sum", "acc", "shift")):
            cols = slice(i0 * P, (i0 + n) * P)
            wide = [P, LISTS, n * P]
            piece_scaled = own(wide, F32, f"scaled{LAST}{i0}")
            piece_tops = own(wide, F32, f"tops{LAST}{i0}")
            piece_shifted = own([P, n * P], F32, f"shifted{LAST}{i0}")
            nc.vector.tensor_tensor(
                piece_scaled[:], fetched[LAST, i0][:], accs["g", LAST][:, cols].unsqueeze(1).to_broadcast(wide),
                ALU.mult,
            )
            nc.vector.scalar_tensor_tensor(
                out=piece_tops[:], in0=accs["s", LAST][:, cols].unsqueeze(1).to_broadcast(wide), scalar=-1.0,
                in1=piece_scaled[:], op0=ALU.mult, op1=ALU.max,
            )
            nc.vector.scalar_tensor_tensor(
                out=piece_shifted[:], in0=accs["s", LAST][:, cols], scalar=float(LISTS), in1=piece_tops[:, 0, :],
                op0=ALU.mult, op1=ALU.add,
            )
            add_up(LAST, i0, n, [piece_tops[:, 1, :], piece_tops[:, 2, :], piece_shifted[:]], ring)

        y_last = own([P, T], F32, "y3")
        for i0, n in PIECES:
            nc.scalar.copy(
                out=pairs[:, i0 : i0 + n, :, LAST * WORDS_A_BLOCK :, :],
                in_=sums[LAST, i0][:, :n, :].rearrange("v i (l u e) -> v i u l e", u=2, e=2),
            )
            if i0 == PIECES[0][0]:
                store_rows(1, 0, CHUNKS, own([P, T], F32, "y1", after=f"tops{LAST}{i0}")[:], "scalar", "back")
        for i0, n in PIECES:
            nc.vector.tensor_copy(out=turned[LAST][:, i0 : i0 + n, :], in_=sums[LAST, i0][:, :n, :])
        store_rows(2, 0, CHUNKS, own([P, T], F32, "y2", after=f"scaled{LAST}{PIECES[-1][0]}")[:], "vector", "sum")
        for i, ring in enumerate(("back", "back", "acc", "acc")):
            planes(i, ring)
            if i % 2 == 1:
                half = slice((i - 1) * P, (i + 1) * P)
                nc.sync.dma_start(out=out_words[:, half], in_=y_codes[:, half].bitcast(I32))
        for i0, ring in ((0, "sum"), (2, "shift")):
            store_rows(LAST, i0, 2, y_last[:, i0 * P : (i0 + 2) * P], "scalar", ring)
        for q in range(QUADRANTS):
            queue = nc.sync if q % 2 == 0 else nc.scalar
            queue.dma_start(
                out=out_2[0, 4 * q : 4 * q + 4, :].bitcast(I32),
                in_=y_scales[32 * q : 32 * q + 4, :].bitcast(I32),
            )
